import numpy as np
import ml_dtypes


def mxq(x, axis, fmt="e4m3"):
    dtype, down = {"e4m3": (ml_dtypes.float8_e4m3fn, 7), "e5m2": (ml_dtypes.float8_e5m2, 14)}[fmt]
    v = np.moveaxis(np.asarray(x, np.float32).astype(ml_dtypes.bfloat16).astype(np.float64), axis, -1)
    blocks = v.reshape(v.shape[:-1] + (-1, 32))
    amax = np.abs(blocks).max(-1, keepdims=True)
    byte = np.maximum(np.where(amax > 0, np.frexp(amax)[1] - 1 + 127, 0) - down, 1)
    scale = np.exp2(byte - 127.0)
    codes = (blocks / scale).astype(np.float32).astype(dtype).astype(np.float64)
    return np.moveaxis((codes * scale).reshape(v.shape), -1, axis)


WIDE = False


def mx_kscale(k):
    if not WIDE:
        return np.ones(k)
    levels = np.array([10, -10, 5, -5, 0])
    if k % 512:
        return np.exp2(np.random.permutation(np.resize(levels, k // 32))).repeat(32)
    a = np.empty((k // 512, 16))
    for p in range(k // 512):
        a[p, :8] = np.random.permutation(np.resize(levels, 8))
        for g in range(8):
            far = levels[np.abs(levels - a[p, g]) >= 10]
            a[p, g + 8] = far[np.random.randint(len(far))]
    return np.exp2(a.ravel()).repeat(32)


def f64(x):
    return np.asarray(x).astype(np.float64)


def striped(idx):
    return np.tile(idx.reshape(-1, 16).T, (8, 1)).astype(np.uint16)


def unstriped(offs):
    return offs[:16].T.reshape(-1).astype(np.int64)


E2M1 = np.array([0.0, 0.5, 1.0, 1.5, 2.0, 3.0, 4.0, 6.0, -0.0, -0.5, -1.0, -1.5, -2.0, -3.0, -4.0, -6.0])


def pack_weight(w, fmt):
    k, n = w.shape
    w = f64(np.asarray(w, np.float32).astype(ml_dtypes.bfloat16)).reshape(k // 32, 32, n)
    amax = np.abs(w).max(1)
    if fmt == "e4m3":
        byte = np.frexp(amax)[1] - 1 + 127 - 7
    else:
        mant, ex = np.frexp(amax / 6.0)
        byte = np.where(mant > 0.5, ex, ex - 1) + 127
    byte = np.clip(np.where(amax > 0, byte, 1), 1, 254)
    scaled = (w * np.exp2(127.0 - byte)[:, None, :]).reshape(k, n).astype(np.float32)
    by_word = np.ascontiguousarray(scaled.reshape(k // 512, 128, 4, n).transpose(0, 1, 3, 2))
    if fmt == "e4m3":
        words = by_word.astype(ml_dtypes.float8_e4m3fn).view(np.uint8)
    else:
        c = by_word.astype(ml_dtypes.float4_e2m1fn).view(np.uint8) & 0xF
        words = (c[..., 0::2] | (c[..., 1::2] << 4)).reshape(k // 512, 128, 2 * n)
    return np.ascontiguousarray(words), np.ascontiguousarray(byte.astype(np.uint8).reshape(k // 512, 16, n))


def unpack_weight(words, scales, fmt):
    g, _, n = scales.shape
    words = np.ascontiguousarray(words).reshape(g, 128, n, -1)
    if fmt == "e4m3":
        vals = words.view(ml_dtypes.float8_e4m3fn).astype(np.float64)
    else:
        nib = np.empty((g, 128, n, 4), np.uint8)
        nib[..., 0::2] = words & 0xF
        nib[..., 1::2] = words >> 4
        vals = E2M1[nib]
    vals = vals * np.repeat(np.exp2(scales.astype(np.float64) - 127.0), 8, axis=1)[..., None]
    return vals.transpose(0, 1, 3, 2).reshape(g * 512, n)


def relu2(v):
    return np.maximum(v, 0.0) ** 2


K, T, E, C, H, N = 512, 512, 4, 256, 512, 128


def by_expert(wq, xq):
    return np.concatenate([wq[e].T @ xq[:, e * C:(e + 1) * C] for e in range(E)], axis=1)


def setup_inputs():
    n = np.random.standard_normal
    s = mx_kscale(K)[:, None]
    u = mx_kscale(H)
    first = np.random.permutation(np.repeat(np.arange(E), T // E))
    second = (first + 1 + np.random.permutation(np.repeat(np.arange(E - 1), -(-T // (E - 1)))[:T])) % E
    while np.bincount(second, minlength=E).max() != T // E:
        load = np.bincount(second, minlength=E); hi, lo = int(load.argmax()), int(load.argmin())
        t = np.flatnonzero((second == hi) & (first != lo))[0]; second[t] = lo
    slot_token = np.empty(E * C, np.int64); pos = np.empty((2, T), np.int64); fill = np.zeros(E, np.int64)
    place = np.stack([np.random.permutation(C) for _ in range(E)])
    for r, deal in enumerate((first, second)):
        for t in np.random.permutation(T):
            e = deal[t]; j = e * C + place[e, fill[e]]; fill[e] += 1; slot_token[j] = t; pos[r, t] = j
    g = np.random.uniform(0.2, 0.8, T)
    w1 = [pack_weight(m, "e2m1") for m in n((E + 1, K, H)) / np.sqrt(K) / s[None] * u[None, None, :]]
    w2 = [pack_weight(m, "e2m1") for m in n((E + 1, H, N)) / np.sqrt(H) / u[None, :, None] ** 2]
    x = pack_weight(n((K, T)) * s, "e4m3")
    return {
        "x_words": x[0],
        "x_scales": x[1],
        "w1_words": np.stack([m[0] for m in w1]),
        "w1_scales": np.stack([m[1] for m in w1]),
        "w2_words": np.stack([m[0] for m in w2]),
        "w2_scales": np.stack([m[1] for m in w2]),
        "gate": np.stack([np.tile(g, (N, 1)), np.tile(1.0 - g, (N, 1))]).astype(np.float32),
        "offs": striped(slot_token),
        "pos1": striped(pos[0]),
        "pos2": striped(pos[1]),
    }


def reference(x_words, x_scales, w1_words, w1_scales, w2_words, w2_scales, gate, offs, pos1, pos2):
    idx = unstriped(offs)
    w1 = np.stack([unpack_weight(w1_words[e], w1_scales[e], "e2m1") for e in range(E + 1)])
    w2 = np.stack([unpack_weight(w2_words[e], w2_scales[e], "e2m1") for e in range(E + 1)])
    w1q, w2q = w1, w2
    xs = unpack_weight(x_words, x_scales, "e4m3")
    hs = relu2(w1q[E].T @ xs)
    ys = w2q[E].T @ mxq(hs, 0, "e4m3")
    xq = unpack_weight(x_words, x_scales, "e4m3")[:, idx]
    h = relu2(by_expert(w1q, xq))
    y = by_expert(w2q, mxq(h, 0, "e4m3"))
    return ys + f64(gate[0]) * y[:, unstriped(pos1)] + f64(gate[1]) * y[:, unstriped(pos2)]

@@ -1,0 +1,229 @@
+from contextlib import ExitStack
+
+import concourse.mybir as mybir
+
+K, T, E, C, H, N = 512, 512, 4, 256, 512, 128
+S = E * C
+FLOPS = 2 * (S + T) * (K * H + H * N)
+
+F32 = mybir.dt.float32
+BF16 = mybir.dt.bfloat16
+I32 = mybir.dt.int32
+U32 = mybir.dt.uint32
+U16 = mybir.dt.uint16
+U8 = mybir.dt.uint8
+FP8X4 = mybir.dt.float8_e4m3fn_x4
+FP4X4 = mybir.dt.float4_e2m1fn_x4
+ACT = mybir.ActivationFunctionType
+ALU = mybir.AluOpType
+
+P = 128
+PACK = 4
+COLS = 128
+SHARED = E
+
+
+def tile_moe_shr_mlp_relu2_kernel(
+    tc, x_words, x_scales, w1_words, w1_scales, w2_words, w2_scales, gate, offs, pos1, pos2, out
+):
+    nc = tc.nc
+    with ExitStack() as ctx:
+        keep = ctx.enter_context(tc.tile_pool(name="keep", bufs=1))
+        ps1 = ctx.enter_context(tc.psum_pool(name="ps1", bufs=4))
+        ps2 = ctx.enter_context(tc.psum_pool(name="ps2", bufs=1))
+        ps3 = ctx.enter_context(tc.psum_pool(name="ps3", bufs=1))
+
+        def tile(shape, dtype, name):
+            return keep.tile(shape, dtype, name=name, align_bytes=64)
+
+        xw = tile([P, T], U32, "xw")
+        xs = tile([P, T], U8, "xs")
+        w1s_raw = tile([P, E + 1, H], U8, "w1s_raw")
+        w2s = tile([P, (E + 1) * N], U8, "w2s")
+        w2w = tile([P, E + 1, 2 * N], U8, "w2w")
+        offs_sb = tile([P, S // 16], U16, "offs_sb")
+        pos1_sb = tile([P, T // 16], U16, "pos1_sb")
+        pos2_sb = tile([P, T // 16], U16, "pos2_sb")
+        gates = tile([P, 2, T], F32, "gates")
+        warm = tile([P, 8], F32, "warm")
+        warm2 = tile([P, 8], F32, "warm2")
+
+        nc.vector.memset(w1s_raw[:].rearrange("p e i -> p (e i)").bitcast(I32), 0)
+        nc.gpsimd.memset(xs[:].bitcast(I32), 0)
+        nc.vector.memset(w2s[:].bitcast(I32), 0)
+        nc.gpsimd.memset(warm[:], 0.0)
+        nc.scalar.activation(warm2[:], warm[:], ACT.Square)
+
+        def load_w1_words(e0, e1):
+            raw = tile([P, e1 - e0, 2 * H], U8, "w1w_raw%d" % e0)
+            nc.sync.dma_start(raw[:].bitcast(I32), w1_words[e0:e1, 0].rearrange("e p b -> p e b").bitcast(I32))
+            return [raw[:, e - e0, :] for e in range(e0, e1)]
+
+        def load_scale_rows(plane, rows, r):
+            nc.sync.dma_start(plane[r:P:32].bitcast(I32), rows[r].bitcast(I32))
+
+        x_rows = x_scales[0].rearrange("(q r) t -> r q t", r=4)
+        w1_rows = w1_scales.rearrange("e s (q r) i -> r q (e s) i", r=4)
+        w2_rows = w2_scales.rearrange("e s (q r) n -> r q (e s) n", r=4)
+        w2s_view = w2s[:].rearrange("p (e n) -> p e n", n=N)
+
+        w1w_raw = {}
+        nc.sync.dma_start(offs_sb[:], offs)
+        w1w_raw[SHARED] = load_w1_words(SHARED, SHARED + 1)[0]
+        nc.sync.dma_start(xw[:].bitcast(I32), x_words[0].rearrange("p t r -> p (t r)").bitcast(I32))
+        for r in range(4):
+            load_scale_rows(w1s_raw[:], w1_rows, r)
+        for r in range(4):
+            load_scale_rows(xs[:], x_rows, r)
+        for e0 in (0, 2):
+            for e, raw in zip((e0, e0 + 1), load_w1_words(e0, e0 + 2)):
+                w1w_raw[e] = raw
+        nc.sync.dma_start(w2w[:].bitcast(I32), w2_words[:, 0].rearrange("e p b -> p e b").bitcast(I32))
+        for r in range(4):
+            load_scale_rows(w2s_view, w2_rows, r)
+        nc.sync.dma_start(pos1_sb[:], pos1)
+        nc.sync.dma_start(pos2_sb[:], pos2)
+        nc.sync.dma_start(gates[:], gate.rearrange("g p t -> p g t"))
+
+        w1w, w1s, xgw, xgs = {}, {}, {}, {}
+
+        def permute_w1(e):
+            w1w[e] = tile([P, 2 * H], U8, "w1w%d" % e)
+            nc.vector.tensor_copy(
+                w1w[e][:].bitcast(U16).rearrange("p (t a b) -> p a t b", t=PACK, b=8),
+                w1w_raw[e].bitcast(U16).rearrange("p (a b t) -> p a t b", t=PACK, b=8),
+            )
+            w1s[e] = tile([P, H], U8, "w1s%d" % e)
+            nc.vector.tensor_copy(
+                w1s[e][:].rearrange("p (t a b) -> p a t b", t=PACK, b=16),
+                w1s_raw[:, e, :].rearrange("p (a b t) -> p a t b", t=PACK, b=16),
+            )
+
+        def gather_words(e):
+            xgw[e] = tile([P, C], U32, "xgw%d" % e)
+            nc.vector.tensor_copy(xgw[e][:], xw[:].indirect(offs_sb[:, e * C // 16 : (e + 1) * C // 16]))
+
+        def gather_scales(e):
+            xgs[e] = tile([P, C], U8, "xgs%d" % e)
+            nc.vector.tensor_copy(xgs[e][:], xs[:].indirect(offs_sb[:, e * C // 16 : (e + 1) * C // 16]))
+
+        y = tile([P, S], F32, "y")
+        relu, hid, acc_shared = {}, {}, {}
+
+        def first_layer(name, e, words, scales, width):
+            relu[name] = tile([P, width * PACK], F32, "relu_%s" % name)
+            for c0 in range(0, width, COLS):
+                acc = ps1.tile([P, PACK, COLS], F32, name="acc1")
+                for t in range(PACK):
+                    nc.tensor.matmul_mx(
+                        out=acc[:, t, :],
+                        lhsT=w1w[e][:, 2 * P * t : 2 * P * (t + 1)].bitcast(FP4X4),
+                        lhsT_scale=w1s[e][:, P * t : P * (t + 1)],
+                        rhs=words[:, c0 : c0 + COLS].bitcast(FP8X4),
+                        rhs_scale=scales[:, c0 : c0 + COLS],
+                        start=True,
+                        stop=True,
+                    )
+                nc.scalar.activation(
+                    relu[name][:, c0 * PACK : (c0 + COLS) * PACK].rearrange("p (c t) -> p c t", t=PACK),
+                    acc[:].rearrange("p t c -> p c t"),
+                    ACT.Relu,
+                )
+
+        def square(name, width, on_vector):
+            hid[name] = tile([P, width * PACK], BF16, "hid_%s" % name)
+            if on_vector:
+                nc.vector.tensor_tensor(hid[name][:], relu[name][:], relu[name][:], ALU.mult)
+            else:
+                nc.scalar.activation(hid[name][:], relu[name][:], ACT.Square)
+
+        def second_layer(name, e, width, acc):
+            codes = tile([P, width], U32, "hw_%s" % name)
+            scales = tile([P, width], U8, "hs_%s" % name)
+            nc.vector.quantize_mx(out=codes[:].bitcast(FP8X4), scales=scales[:], in_=hid[name][:])
+            nc.tensor.matmul_mx(
+                out=acc,
+                lhsT=w2w[:, e, :].bitcast(FP4X4),
+                lhsT_scale=w2s[:, e * N : (e + 1) * N],
+                rhs=codes[:].bitcast(FP8X4),
+                rhs_scale=scales[:],
+                start=True,
+                stop=True,
+            )
+
+        def shared_first(name, c0, width):
+            first_layer(name, SHARED, xw[:, c0 : c0 + width], xs[:, c0 : c0 + width], width)
+
+        def shared_second(name, width):
+            acc_shared[name] = ps3.tile([P, width], F32, name="acc_%s" % name)
+            second_layer(name, SHARED, width, acc_shared[name][:])
+
+        def routed_first(name, e, c0, width):
+            first_layer(name, e, xgw[e][:, c0 : c0 + width], xgs[e][:, c0 : c0 + width], width)
+
+        def routed_second(name, e, c0, width):
+            acc = ps2.tile([P, width], F32, name="acc2")
+            second_layer(name, e, width, acc[:])
+            nc.vector.tensor_copy(y[:, e * C + c0 : e * C + c0 + width], acc[:])
+
+        permute_w1(SHARED)
+        gather_words(0)
+        shared_first("s0", 0, COLS)
+        gather_scales(0)
+        permute_w1(0)
+        square("s0", COLS, False)
+        gather_words(1)
+        routed_first("e0", 0, 0, C)
+        gather_scales(1)
+        permute_w1(1)
+        square("e0", C, False)
+        gather_words(2)
+        shared_second("s0", COLS)
+        routed_first("e1", 1, 0, C)
+        gather_scales(2)
+        permute_w1(2)
+        square("e1", C, False)
+        gather_words(3)
+        routed_second("e0", 0, 0, C)
+        routed_first("e2", 2, 0, C)
+        gather_scales(3)
+        permute_w1(3)
+        routed_second("e1", 1, 0, C)
+        routed_first("e3a", 3, 0, COLS)
+        routed_first("e3b", 3, COLS, COLS)
+        square("e2", C, True)
+        square("e3a", COLS, False)
+        square("e3b", COLS, False)
+        routed_second("e2", 2, 0, C)
+        routed_second("e3a", 3, 0, COLS)
+        shared_first("s1", COLS, C)
+        routed_second("e3b", 3, COLS, COLS)
+        square("s1", C, False)
+        shared_first("s2", COLS + C, COLS)
+        square("s2", COLS, False)
+
+        def combine(half):
+            cols = slice(half * C, (half + 1) * C)
+            lists = slice(half * C // 16, (half + 1) * C // 16)
+            first = tile([P, C], F32, "first%d" % half)
+            second = tile([P, C], F32, "second%d" % half)
+            nc.vector.tensor_tensor(first[:], y[:].indirect(pos1_sb[:, lists]), gates[:, 0, cols], ALU.mult)
+            nc.vector.tensor_tensor(second[:], y[:].indirect(pos2_sb[:, lists]), gates[:, 1, cols], ALU.mult)
+            return first, second
+
+        routed = tile([P, T], F32, "routed")
+
+        def finish(name, c0, width):
+            total = tile([P, width], F32, "total_%s" % name)
+            nc.vector.tensor_tensor(total[:], acc_shared[name][:], routed[:, c0 : c0 + width], ALU.add)
+            nc.sync.dma_start(out[:, c0 : c0 + width], total[:])
+
+        first, second = combine(0)
+        shared_second("s1", C)
+        nc.vector.tensor_tensor(routed[:, :C], first[:], second[:], ALU.add)
+        first, second = combine(1)
+        finish("s0", 0, COLS)
+        shared_second("s2", COLS)
+        nc.vector.tensor_tensor(routed[:, C:], first[:], second[:], ALU.add)
+        finish("s1", COLS, C)
+        finish("s2", COLS + C, COLS)

@@ -30,11 +30,18 @@ def tile_moe_shr_mlp_relu2_kernel(
     with ExitStack() as ctx:
         keep = ctx.enter_context(tc.tile_pool(name="keep", bufs=1))
         ps1 = ctx.enter_context(tc.psum_pool(name="ps1", bufs=4))
-        ps2 = ctx.enter_context(tc.psum_pool(name="ps2", bufs=1))
+        ps2 = ctx.enter_context(tc.psum_pool(name="ps2", bufs=2))
         ps3 = ctx.enter_context(tc.psum_pool(name="ps3", bufs=1))
+
+        ring = ctx.enter_context(tc.tile_pool(name="ring", bufs=2))
 
         def tile(shape, dtype, name):
             return keep.tile(shape, dtype, name=name, align_bytes=64)
+
+        def prep_tile(shape, dtype, name, e):
+            if e == SHARED:
+                return tile(shape, dtype, name + "_shared")
+            return ring.tile(shape, dtype, name=name, align_bytes=64)
 
         xw = tile([P, T], U32, "xw")
         xs = tile([P, T], U8, "xs")
@@ -54,10 +61,12 @@ def tile_moe_shr_mlp_relu2_kernel(
         nc.gpsimd.memset(warm[:], 0.0)
         nc.scalar.activation(warm2[:], warm[:], ACT.Square)
 
-        def load_w1_words(e0, e1):
-            raw = tile([P, e1 - e0, 2 * H], U8, "w1w_raw%d" % e0)
-            nc.sync.dma_start(raw[:].bitcast(I32), w1_words[e0:e1, 0].rearrange("e p b -> p e b").bitcast(I32))
-            return [raw[:, e - e0, :] for e in range(e0, e1)]
+        def load_w1_words(experts):
+            raw = tile([P, len(experts), 2 * H], U8, "w1w_raw%d" % experts[0])
+            rows = w1_words[experts.start : experts.stop : experts.step, 0]
+            nc.sync.dma_start(raw[:].bitcast(I32), rows.rearrange("e p b -> p e b").bitcast(I32))
+            for n, e in enumerate(experts):
+                w1w_raw[e] = raw[:, n, :]
 
         def load_scale_rows(plane, rows, r):
             nc.sync.dma_start(plane[r:P:32].bitcast(I32), rows[r].bitcast(I32))
@@ -69,15 +78,13 @@ def tile_moe_shr_mlp_relu2_kernel(
 
         w1w_raw = {}
         nc.sync.dma_start(offs_sb[:], offs)
-        w1w_raw[SHARED] = load_w1_words(SHARED, SHARED + 1)[0]
         nc.sync.dma_start(xw[:].bitcast(I32), x_words[0].rearrange("p t r -> p (t r)").bitcast(I32))
+        load_w1_words(range(0, E + 1, E))
         for r in range(4):
             load_scale_rows(w1s_raw[:], w1_rows, r)
         for r in range(4):
             load_scale_rows(xs[:], x_rows, r)
-        for e0 in (0, 2):
-            for e, raw in zip((e0, e0 + 1), load_w1_words(e0, e0 + 2)):
-                w1w_raw[e] = raw
+        load_w1_words(range(1, E))
         nc.sync.dma_start(w2w[:].bitcast(I32), w2_words[:, 0].rearrange("e p b -> p e b").bitcast(I32))
         for r in range(4):
             load_scale_rows(w2s_view, w2_rows, r)
@@ -88,23 +95,23 @@ def tile_moe_shr_mlp_relu2_kernel(
         w1w, w1s, xgw, xgs = {}, {}, {}, {}
 
         def permute_w1(e):
-            w1w[e] = tile([P, 2 * H], U8, "w1w%d" % e)
+            w1w[e] = prep_tile([P, 2 * H], U8, "w1w", e)
             nc.vector.tensor_copy(
                 w1w[e][:].bitcast(U16).rearrange("p (t a b) -> p a t b", t=PACK, b=8),
                 w1w_raw[e].bitcast(U16).rearrange("p (a b t) -> p a t b", t=PACK, b=8),
             )
-            w1s[e] = tile([P, H], U8, "w1s%d" % e)
+            w1s[e] = prep_tile([P, H], U8, "w1s", e)
             nc.vector.tensor_copy(
                 w1s[e][:].rearrange("p (t a b) -> p a t b", t=PACK, b=16),
                 w1s_raw[:, e, :].rearrange("p (a b t) -> p a t b", t=PACK, b=16),
             )
 
         def gather_words(e):
-            xgw[e] = tile([P, C], U32, "xgw%d" % e)
+            xgw[e] = prep_tile([P, C], U32, "xgw", e)
             nc.vector.tensor_copy(xgw[e][:], xw[:].indirect(offs_sb[:, e * C // 16 : (e + 1) * C // 16]))
 
         def gather_scales(e):
-            xgs[e] = tile([P, C], U8, "xgs%d" % e)
+            xgs[e] = prep_tile([P, C], U8, "xgs", e)
             nc.vector.tensor_copy(xgs[e][:], xs[:].indirect(offs_sb[:, e * C // 16 : (e + 1) * C // 16]))
 
         y = tile([P, S], F32, "y")
@@ -161,69 +168,67 @@ def tile_moe_shr_mlp_relu2_kernel(
         def routed_first(name, e, c0, width):
             first_layer(name, e, xgw[e][:, c0 : c0 + width], xgs[e][:, c0 : c0 + width], width)
 
-        def routed_second(name, e, c0, width):
+        def routed_second(name, e, c0, width, on_vector):
             acc = ps2.tile([P, width], F32, name="acc2")
             second_layer(name, e, width, acc[:])
-            nc.vector.tensor_copy(y[:, e * C + c0 : e * C + c0 + width], acc[:])
-
-        permute_w1(SHARED)
-        gather_words(0)
-        shared_first("s0", 0, COLS)
-        gather_scales(0)
-        permute_w1(0)
-        square("s0", COLS, False)
-        gather_words(1)
-        routed_first("e0", 0, 0, C)
-        gather_scales(1)
-        permute_w1(1)
-        square("e0", C, False)
-        gather_words(2)
-        shared_second("s0", COLS)
-        routed_first("e1", 1, 0, C)
-        gather_scales(2)
-        permute_w1(2)
-        square("e1", C, False)
-        gather_words(3)
-        routed_second("e0", 0, 0, C)
-        routed_first("e2", 2, 0, C)
-        gather_scales(3)
-        permute_w1(3)
-        routed_second("e1", 1, 0, C)
-        routed_first("e3a", 3, 0, COLS)
-        routed_first("e3b", 3, COLS, COLS)
-        square("e2", C, True)
-        square("e3a", COLS, False)
-        square("e3b", COLS, False)
-        routed_second("e2", 2, 0, C)
-        routed_second("e3a", 3, 0, COLS)
-        shared_first("s1", COLS, C)
-        routed_second("e3b", 3, COLS, COLS)
-        square("s1", C, False)
-        shared_first("s2", COLS + C, COLS)
-        square("s2", COLS, False)
-
-        def combine(half):
-            cols = slice(half * C, (half + 1) * C)
-            lists = slice(half * C // 16, (half + 1) * C // 16)
-            first = tile([P, C], F32, "first%d" % half)
-            second = tile([P, C], F32, "second%d" % half)
-            nc.vector.tensor_tensor(first[:], y[:].indirect(pos1_sb[:, lists]), gates[:, 0, cols], ALU.mult)
-            nc.vector.tensor_tensor(second[:], y[:].indirect(pos2_sb[:, lists]), gates[:, 1, cols], ALU.mult)
-            return first, second
+            slots = y[:, e * C + c0 : e * C + c0 + width]
+            if on_vector:
+                nc.vector.tensor_copy(slots, acc[:])
+            else:
+                nc.scalar.copy(slots, acc[:])
 
         routed = tile([P, T], F32, "routed")
+
+        def fetch(which, c0, width):
+            picked = tile([P, width], F32, "picked%d_%d" % (which, c0))
+            lists = (pos1_sb, pos2_sb)[which][:, c0 // 16 : (c0 + width) // 16]
+            nc.vector.tensor_tensor(picked[:], y[:].indirect(lists), gates[:, which, c0 : c0 + width], ALU.mult)
+            return picked
 
         def finish(name, c0, width):
             total = tile([P, width], F32, "total_%s" % name)
             nc.vector.tensor_tensor(total[:], acc_shared[name][:], routed[:, c0 : c0 + width], ALU.add)
             nc.sync.dma_start(out[:, c0 : c0 + width], total[:])
 
-        first, second = combine(0)
+        gather_words(0)
+        permute_w1(SHARED)
+        shared_first("s0", 0, C)
+        permute_w1(0)
+        gather_scales(0)
+        gather_words(1)
+        routed_first("e0", 0, 0, C)
+        gather_scales(1)
+        permute_w1(1)
+        square("e0", C, False)
+        routed_first("e1", 1, 0, C)
+        gather_words(2)
+        gather_scales(2)
+        permute_w1(2)
+        square("e1", C, False)
+        routed_first("e2a", 2, 0, COLS)
+        routed_first("e2b", 2, COLS, COLS)
+        gather_words(3)
+        gather_scales(3)
+        permute_w1(3)
+        routed_first("e3a", 3, 0, COLS)
+        routed_first("e3b", 3, COLS, COLS)
+        routed_second("e0", 0, 0, C, False)
+        routed_second("e1", 1, 0, C, False)
+        square("e2a", COLS, True)
+        square("e2b", COLS, True)
+        square("e3a", COLS, True)
+        square("e3b", COLS, True)
+        routed_second("e2a", 2, 0, COLS, False)
+        routed_second("e2b", 2, COLS, COLS, False)
+        routed_second("e3a", 3, 0, COLS, False)
+        routed_second("e3b", 3, COLS, COLS, False)
+        square("s0", C, False)
+        shared_second("s0", C)
+        shared_first("s1", C, C)
+        square("s1", C, False)
+        a = fetch(0, 0, T)
+        b = fetch(1, 0, T)
         shared_second("s1", C)
-        nc.vector.tensor_tensor(routed[:, :C], first[:], second[:], ALU.add)
-        first, second = combine(1)
-        finish("s0", 0, COLS)
-        shared_second("s2", COLS)
-        nc.vector.tensor_tensor(routed[:, C:], first[:], second[:], ALU.add)
-        finish("s1", COLS, C)
-        finish("s2", COLS + C, COLS)
+        nc.vector.tensor_tensor(routed[:], a[:], b[:], ALU.add)
+        finish("s0", 0, C)
+        finish("s1", C, C)

@@ -1,6 +1,7 @@
 from contextlib import ExitStack
 
 import concourse.mybir as mybir
+from concourse.masks import make_identity
 
 K, T, E, C, H, N = 512, 512, 4, 256, 512, 128
 S = E * C
@@ -21,6 +22,7 @@ P = 128
 PACK = 4
 COLS = 128
 SHARED = E
+REUSE = {}
 
 
 def tile_moe_shr_mlp_relu2_kernel(
@@ -30,7 +32,7 @@ def tile_moe_shr_mlp_relu2_kernel(
     with ExitStack() as ctx:
         keep = ctx.enter_context(tc.tile_pool(name="keep", bufs=1))
         ps1 = ctx.enter_context(tc.psum_pool(name="ps1", bufs=4))
-        ps2 = ctx.enter_context(tc.psum_pool(name="ps2", bufs=2))
+        ps2 = ctx.enter_context(tc.psum_pool(name="ps2", bufs=3))
         ps3 = ctx.enter_context(tc.psum_pool(name="ps3", bufs=1))
 
         ring = ctx.enter_context(tc.tile_pool(name="ring", bufs=2))
@@ -60,6 +62,9 @@ def tile_moe_shr_mlp_relu2_kernel(
         nc.vector.memset(w2s[:].bitcast(I32), 0)
         nc.gpsimd.memset(warm[:], 0.0)
         nc.scalar.activation(warm2[:], warm[:], ACT.Square)
+
+        ident = tile([P, P], F32, "ident")
+        make_identity(nc, ident[:])
 
         def load_w1_words(experts):
             raw = tile([P, len(experts), 2 * H], U8, "w1w_raw%d" % experts[0])
@@ -118,7 +123,7 @@ def tile_moe_shr_mlp_relu2_kernel(
         relu, hid, acc_shared = {}, {}, {}
 
         def first_layer(name, e, words, scales, width):
-            relu[name] = tile([P, width * PACK], F32, "relu_%s" % name)
+            relu[name] = tile([P, width * PACK], F32, "relu_%s" % REUSE.get(name, name))
             for c0 in range(0, width, COLS):
                 acc = ps1.tile([P, PACK, COLS], F32, name="acc1")
                 for t in range(PACK):
@@ -137,12 +142,47 @@ def tile_moe_shr_mlp_relu2_kernel(
                     ACT.Relu,
                 )
 
-        def square(name, width, on_vector):
+        def turned_first(name, e, engines):
+            relu[name] = tile([P, C // COLS, PACK, P], F32, "relu_%s" % name)
+            for n, engine in enumerate(engines):
+                cols = slice(n * COLS, (n + 1) * COLS)
+                acc = ps1.tile([P, H], F32, name="acc1")
+                nc.tensor.matmul_mx(
+                    out=acc[:],
+                    lhsT=xgw[e][:, cols].bitcast(FP8X4),
+                    lhsT_scale=xgs[e][:, cols],
+                    rhs=w1w_raw[e].bitcast(FP4X4),
+                    rhs_scale=w1s_raw[:, e, :],
+                    start=True,
+                    stop=True,
+                )
+                by_plane = acc[:].rearrange("p (m t) -> p t m", t=PACK)
+                if engine is nc.vector:
+                    nc.vector.tensor_scalar_max(relu[name][:, n], by_plane, 0.0)
+                else:
+                    nc.scalar.activation(relu[name][:, n], by_plane, ACT.Relu)
+
+        def turned_square(name):
+            hid[name] = tile([P, C * PACK], BF16, "hid_%s" % name)
+            for n in range(C // COLS):
+                turned = ps1.tile([P, PACK, COLS], F32, name="acc1")
+                for t in range(PACK):
+                    nc.tensor.transpose(turned[:, t, :], relu[name][:, n, t, :], ident[:])
+                nc.scalar.activation(
+                    hid[name][:, n * COLS * PACK : (n + 1) * COLS * PACK].rearrange("p (c t) -> p c t", t=PACK),
+                    turned[:].rearrange("p t c -> p c t"),
+                    ACT.Square,
+                )
+
+        def square(name, width, engines):
             hid[name] = tile([P, width * PACK], BF16, "hid_%s" % name)
-            if on_vector:
-                nc.vector.tensor_tensor(hid[name][:], relu[name][:], relu[name][:], ALU.mult)
-            else:
-                nc.scalar.activation(hid[name][:], relu[name][:], ACT.Square)
+            step = width * PACK // len(engines)
+            for n, engine in enumerate(engines):
+                cols = slice(n * step, (n + 1) * step)
+                if engine is nc.scalar:
+                    nc.scalar.activation(hid[name][:, cols], relu[name][:, cols], ACT.Square)
+                else:
+                    engine.tensor_tensor(hid[name][:, cols], relu[name][:, cols], relu[name][:, cols], ALU.mult)
 
         def second_layer(name, e, width, acc):
             codes = tile([P, width], U32, "hw_%s" % name)
@@ -161,9 +201,11 @@ def tile_moe_shr_mlp_relu2_kernel(
         def shared_first(name, c0, width):
             first_layer(name, SHARED, xw[:, c0 : c0 + width], xs[:, c0 : c0 + width], width)
 
-        def shared_second(name, width):
-            acc_shared[name] = ps3.tile([P, width], F32, name="acc_%s" % name)
-            second_layer(name, SHARED, width, acc_shared[name][:])
+        shared_bank = ps3.tile([P, T], F32, name="shared_bank")
+
+        def shared_second(name, c0, width):
+            acc_shared[name] = shared_bank[:, c0 : c0 + width]
+            second_layer(name, SHARED, width, acc_shared[name])
 
         def routed_first(name, e, c0, width):
             first_layer(name, e, xgw[e][:, c0 : c0 + width], xgs[e][:, c0 : c0 + width], width)
@@ -177,8 +219,6 @@ def tile_moe_shr_mlp_relu2_kernel(
             else:
                 nc.scalar.copy(slots, acc[:])
 
-        routed = tile([P, T], F32, "routed")
-
         def fetch(which, c0, width):
             picked = tile([P, width], F32, "picked%d_%d" % (which, c0))
             lists = (pos1_sb, pos2_sb)[which][:, c0 // 16 : (c0 + width) // 16]
@@ -187,48 +227,44 @@ def tile_moe_shr_mlp_relu2_kernel(
 
         def finish(name, c0, width):
             total = tile([P, width], F32, "total_%s" % name)
-            nc.vector.tensor_tensor(total[:], acc_shared[name][:], routed[:, c0 : c0 + width], ALU.add)
+            nc.vector.tensor_tensor(total[:], acc_shared[name], routed[:, c0 : c0 + width], ALU.add)
             nc.sync.dma_start(out[:, c0 : c0 + width], total[:])
 
         gather_words(0)
         permute_w1(SHARED)
         shared_first("s0", 0, C)
-        permute_w1(0)
         gather_scales(0)
         gather_words(1)
-        routed_first("e0", 0, 0, C)
+        turned_first("e0", 0, [nc.scalar, nc.scalar])
         gather_scales(1)
-        permute_w1(1)
-        square("e0", C, False)
-        routed_first("e1", 1, 0, C)
+        turned_first("e1", 1, [nc.scalar, nc.vector])
+        turned_square("e0")
         gather_words(2)
         gather_scales(2)
         permute_w1(2)
-        square("e1", C, False)
-        routed_first("e2a", 2, 0, COLS)
-        routed_first("e2b", 2, COLS, COLS)
+        routed_first("e2", 2, 0, C)
+        turned_square("e1")
         gather_words(3)
         gather_scales(3)
         permute_w1(3)
         routed_first("e3a", 3, 0, COLS)
         routed_first("e3b", 3, COLS, COLS)
+        square("e2", C, [nc.vector])
+        square("e3a", COLS, [nc.vector])
+        square("e3b", COLS, [nc.scalar])
         routed_second("e0", 0, 0, C, False)
         routed_second("e1", 1, 0, C, False)
-        square("e2a", COLS, True)
-        square("e2b", COLS, True)
-        square("e3a", COLS, True)
-        square("e3b", COLS, True)
-        routed_second("e2a", 2, 0, COLS, False)
-        routed_second("e2b", 2, COLS, COLS, False)
+        routed_second("e2", 2, 0, C, False)
         routed_second("e3a", 3, 0, COLS, False)
-        routed_second("e3b", 3, COLS, COLS, False)
-        square("s0", C, False)
-        shared_second("s0", C)
+        routed_second("e3b", 3, COLS, COLS, True)
+        square("s0", C, [nc.scalar])
+        shared_second("s0", 0, C)
         shared_first("s1", C, C)
-        square("s1", C, False)
+        square("s1", C, [nc.scalar])
         a = fetch(0, 0, T)
         b = fetch(1, 0, T)
-        shared_second("s1", C)
+        shared_second("s1", C, C)
+        routed = tile([P, T], F32, "hid_s1")
         nc.vector.tensor_tensor(routed[:], a[:], b[:], ALU.add)
         finish("s0", 0, C)
         finish("s1", C, C)

@@ -4,8 +4,9 @@ import concourse.mybir as mybir
 from concourse.masks import make_identity
 
 K, T, E, C, H, N = 512, 512, 4, 256, 512, 128
-S = E * C
-FLOPS = 2 * (S + T) * (K * H + H * N)
+SLOTS = E * C
+SHARED = E
+FLOPS = 2 * (SLOTS + T) * (K * H + H * N)
 
 F32 = mybir.dt.float32
 BF16 = mybir.dt.bfloat16
@@ -20,9 +21,13 @@ ALU = mybir.AluOpType
 
 P = 128
 PACK = 4
-COLS = 128
-SHARED = E
-REUSE = {}
+QUAD = 32
+LIVE = 4
+PER_COLUMN = 16
+LINE = 16
+BLOCK = 128
+HALF = T // 2
+TURNED = 2
 
 
 def tile_moe_shr_mlp_relu2_kernel(
@@ -31,240 +36,182 @@ def tile_moe_shr_mlp_relu2_kernel(
     nc = tc.nc
     with ExitStack() as ctx:
         keep = ctx.enter_context(tc.tile_pool(name="keep", bufs=1))
-        ps1 = ctx.enter_context(tc.psum_pool(name="ps1", bufs=4))
-        ps2 = ctx.enter_context(tc.psum_pool(name="ps2", bufs=3))
-        ps3 = ctx.enter_context(tc.psum_pool(name="ps3", bufs=1))
-
         ring = ctx.enter_context(tc.tile_pool(name="ring", bufs=2))
+        psum1 = ctx.enter_context(tc.psum_pool(name="psum1", bufs=5))
+        psum2 = ctx.enter_context(tc.psum_pool(name="psum2", bufs=3))
 
-        def tile(shape, dtype, name):
-            return keep.tile(shape, dtype, name=name, align_bytes=64)
-
-        def prep_tile(shape, dtype, name, e):
-            if e == SHARED:
-                return tile(shape, dtype, name + "_shared")
-            return ring.tile(shape, dtype, name=name, align_bytes=64)
+        def tile(shape, dtype, name, pool=keep):
+            return pool.tile(shape, dtype, name=name, align_bytes=64)
 
         xw = tile([P, T], U32, "xw")
         xs = tile([P, T], U8, "xs")
-        w1s_raw = tile([P, E + 1, H], U8, "w1s_raw")
-        w2s = tile([P, (E + 1) * N], U8, "w2s")
+        w1s = tile([P, E + 1, H], U8, "w1s")
+        w2s = tile([P, E + 1, N], U8, "w2s")
         w2w = tile([P, E + 1, 2 * N], U8, "w2w")
-        offs_sb = tile([P, S // 16], U16, "offs_sb")
-        pos1_sb = tile([P, T // 16], U16, "pos1_sb")
-        pos2_sb = tile([P, T // 16], U16, "pos2_sb")
+        offs_sb = tile([P, SLOTS // PER_COLUMN], U16, "offs_sb")
+        pos1_sb = tile([P, T // PER_COLUMN], U16, "pos1_sb")
+        pos2_sb = tile([P, T // PER_COLUMN], U16, "pos2_sb")
         gates = tile([P, 2, T], F32, "gates")
-        warm = tile([P, 8], F32, "warm")
-        warm2 = tile([P, 8], F32, "warm2")
-
-        nc.vector.memset(w1s_raw[:].rearrange("p e i -> p (e i)").bitcast(I32), 0)
-        nc.gpsimd.memset(xs[:].bitcast(I32), 0)
-        nc.vector.memset(w2s[:].bitcast(I32), 0)
-        nc.gpsimd.memset(warm[:], 0.0)
-        nc.scalar.activation(warm2[:], warm[:], ACT.Square)
-
         ident = tile([P, P], F32, "ident")
+        y = tile([P, SLOTS], F32, "y")
+
+        for plane in (w1s, w2s):
+            nc.vector.memset(plane[:].rearrange("p e c -> p (e c)").bitcast(I32), 0)
         make_identity(nc, ident[:])
 
-        def load_w1_words(experts):
-            raw = tile([P, len(experts), 2 * H], U8, "w1w_raw%d" % experts[0])
-            rows = w1_words[experts.start : experts.stop : experts.step, 0]
-            nc.sync.dma_start(raw[:].bitcast(I32), rows.rearrange("e p b -> p e b").bitcast(I32))
-            for n, e in enumerate(experts):
-                w1w_raw[e] = raw[:, n, :]
+        w1w = {}
 
-        def load_scale_rows(plane, rows, r):
-            nc.sync.dma_start(plane[r:P:32].bitcast(I32), rows[r].bitcast(I32))
+        def load_w1_words(first, last):
+            words = tile([P, last - first, 2 * H], U8, "w1w_from%d" % first)
+            nc.sync.dma_start(words[:].bitcast(I32), w1_words[first:last, 0].rearrange("e p b -> p e b").bitcast(I32))
+            for e in range(first, last):
+                w1w[e] = words[:, e - first, :]
 
-        x_rows = x_scales[0].rearrange("(q r) t -> r q t", r=4)
-        w1_rows = w1_scales.rearrange("e s (q r) i -> r q (e s) i", r=4)
-        w2_rows = w2_scales.rearrange("e s (q r) n -> r q (e s) n", r=4)
-        w2s_view = w2s[:].rearrange("p (e n) -> p e n", n=N)
+        def load_weight_scales(plane, scales):
+            rows = scales.rearrange("e s (q r) c -> r q (e s) c", r=LIVE)
+            for r in range(LIVE):
+                nc.sync.dma_start(plane[r:P:QUAD].bitcast(I32), rows[r].bitcast(I32))
 
-        w1w_raw = {}
         nc.sync.dma_start(offs_sb[:], offs)
+        x_rows = x_scales[0].rearrange("(q r) t -> q r t", r=LIVE).bitcast(I32)
+        for q in range(P // QUAD):
+            repeated = x_rows[q].unsqueeze(0).broadcast_to([QUAD // LIVE, LIVE, T // 4])
+            nc.sync.dma_start(xs[QUAD * q : QUAD * (q + 1), :].bitcast(I32), repeated)
         nc.sync.dma_start(xw[:].bitcast(I32), x_words[0].rearrange("p t r -> p (t r)").bitcast(I32))
-        load_w1_words(range(0, E + 1, E))
-        for r in range(4):
-            load_scale_rows(w1s_raw[:], w1_rows, r)
-        for r in range(4):
-            load_scale_rows(xs[:], x_rows, r)
-        load_w1_words(range(1, E))
+        load_w1_words(0, TURNED)
+        load_weight_scales(w1s[:], w1_scales)
+        load_w1_words(TURNED, E + 1)
         nc.sync.dma_start(w2w[:].bitcast(I32), w2_words[:, 0].rearrange("e p b -> p e b").bitcast(I32))
-        for r in range(4):
-            load_scale_rows(w2s_view, w2_rows, r)
+        load_weight_scales(w2s[:], w2_scales)
         nc.sync.dma_start(pos1_sb[:], pos1)
         nc.sync.dma_start(pos2_sb[:], pos2)
         nc.sync.dma_start(gates[:], gate.rearrange("g p t -> p g t"))
 
-        w1w, w1s, xgw, xgs = {}, {}, {}, {}
+        slot_words, slot_scales, perm_words, perm_scales, relu, hidden = {}, {}, {}, {}, {}, {}
 
-        def permute_w1(e):
-            w1w[e] = prep_tile([P, 2 * H], U8, "w1w", e)
-            nc.vector.tensor_copy(
-                w1w[e][:].bitcast(U16).rearrange("p (t a b) -> p a t b", t=PACK, b=8),
-                w1w_raw[e].bitcast(U16).rearrange("p (a b t) -> p a t b", t=PACK, b=8),
-            )
-            w1s[e] = prep_tile([P, H], U8, "w1s", e)
-            nc.vector.tensor_copy(
-                w1s[e][:].rearrange("p (t a b) -> p a t b", t=PACK, b=16),
-                w1s_raw[:, e, :].rearrange("p (a b t) -> p a t b", t=PACK, b=16),
-            )
+        def expert_entries(e):
+            return offs_sb[:, e * C // PER_COLUMN : (e + 1) * C // PER_COLUMN]
 
         def gather_words(e):
-            xgw[e] = prep_tile([P, C], U32, "xgw", e)
-            nc.vector.tensor_copy(xgw[e][:], xw[:].indirect(offs_sb[:, e * C // 16 : (e + 1) * C // 16]))
+            slot_words[e] = tile([P, C], U32, "slot_words", ring)
+            nc.vector.tensor_copy(slot_words[e][:], xw[:].indirect(expert_entries(e)))
 
         def gather_scales(e):
-            xgs[e] = prep_tile([P, C], U8, "xgs", e)
-            nc.vector.tensor_copy(xgs[e][:], xs[:].indirect(offs_sb[:, e * C // 16 : (e + 1) * C // 16]))
+            slot_scales[e] = tile([P, C], U8, "slot_scales", ring)
+            nc.vector.tensor_copy(slot_scales[e][:], xs[:].indirect(expert_entries(e)))
 
-        y = tile([P, S], F32, "y")
-        relu, hid, acc_shared = {}, {}, {}
-
-        def first_layer(name, e, words, scales, width):
-            relu[name] = tile([P, width * PACK], F32, "relu_%s" % REUSE.get(name, name))
-            for c0 in range(0, width, COLS):
-                acc = ps1.tile([P, PACK, COLS], F32, name="acc1")
-                for t in range(PACK):
-                    nc.tensor.matmul_mx(
-                        out=acc[:, t, :],
-                        lhsT=w1w[e][:, 2 * P * t : 2 * P * (t + 1)].bitcast(FP4X4),
-                        lhsT_scale=w1s[e][:, P * t : P * (t + 1)],
-                        rhs=words[:, c0 : c0 + COLS].bitcast(FP8X4),
-                        rhs_scale=scales[:, c0 : c0 + COLS],
-                        start=True,
-                        stop=True,
-                    )
-                nc.scalar.activation(
-                    relu[name][:, c0 * PACK : (c0 + COLS) * PACK].rearrange("p (c t) -> p c t", t=PACK),
-                    acc[:].rearrange("p t c -> p c t"),
-                    ACT.Relu,
-                )
-
-        def turned_first(name, e, engines):
-            relu[name] = tile([P, C // COLS, PACK, P], F32, "relu_%s" % name)
-            for n, engine in enumerate(engines):
-                cols = slice(n * COLS, (n + 1) * COLS)
-                acc = ps1.tile([P, H], F32, name="acc1")
-                nc.tensor.matmul_mx(
-                    out=acc[:],
-                    lhsT=xgw[e][:, cols].bitcast(FP8X4),
-                    lhsT_scale=xgs[e][:, cols],
-                    rhs=w1w_raw[e].bitcast(FP4X4),
-                    rhs_scale=w1s_raw[:, e, :],
-                    start=True,
-                    stop=True,
-                )
-                by_plane = acc[:].rearrange("p (m t) -> p t m", t=PACK)
-                if engine is nc.vector:
-                    nc.vector.tensor_scalar_max(relu[name][:, n], by_plane, 0.0)
-                else:
-                    nc.scalar.activation(relu[name][:, n], by_plane, ACT.Relu)
-
-        def turned_square(name):
-            hid[name] = tile([P, C * PACK], BF16, "hid_%s" % name)
-            for n in range(C // COLS):
-                turned = ps1.tile([P, PACK, COLS], F32, name="acc1")
-                for t in range(PACK):
-                    nc.tensor.transpose(turned[:, t, :], relu[name][:, n, t, :], ident[:])
-                nc.scalar.activation(
-                    hid[name][:, n * COLS * PACK : (n + 1) * COLS * PACK].rearrange("p (c t) -> p c t", t=PACK),
-                    turned[:].rearrange("p t c -> p c t"),
-                    ACT.Square,
-                )
-
-        def square(name, width, engines):
-            hid[name] = tile([P, width * PACK], BF16, "hid_%s" % name)
-            step = width * PACK // len(engines)
-            for n, engine in enumerate(engines):
-                cols = slice(n * step, (n + 1) * step)
-                if engine is nc.scalar:
-                    nc.scalar.activation(hid[name][:, cols], relu[name][:, cols], ACT.Square)
-                else:
-                    engine.tensor_tensor(hid[name][:, cols], relu[name][:, cols], relu[name][:, cols], ALU.mult)
-
-        def second_layer(name, e, width, acc):
-            codes = tile([P, width], U32, "hw_%s" % name)
-            scales = tile([P, width], U8, "hs_%s" % name)
-            nc.vector.quantize_mx(out=codes[:].bitcast(FP8X4), scales=scales[:], in_=hid[name][:])
-            nc.tensor.matmul_mx(
-                out=acc,
-                lhsT=w2w[:, e, :].bitcast(FP4X4),
-                lhsT_scale=w2s[:, e * N : (e + 1) * N],
-                rhs=codes[:].bitcast(FP8X4),
-                rhs_scale=scales[:],
-                start=True,
-                stop=True,
+        def reorder(dst, src, run):
+            nc.vector.tensor_copy(
+                dst.rearrange("p (t a b) -> p a t b", t=PACK, b=run),
+                src.rearrange("p (a b t) -> p a t b", t=PACK, b=run),
             )
 
-        def shared_first(name, c0, width):
-            first_layer(name, SHARED, xw[:, c0 : c0 + width], xs[:, c0 : c0 + width], width)
+        def permute_w1(e):
+            perm_words[e] = tile([P, 2 * H], U8, "perm_words", ring)
+            reorder(perm_words[e][:].bitcast(U16), w1w[e].bitcast(U16), LINE // 2)
+            perm_scales[e] = tile([P, H], U8, "perm_scales", ring)
+            reorder(perm_scales[e][:], w1s[:, e, :], LINE)
 
-        shared_bank = ps3.tile([P, T], F32, name="shared_bank")
+        def mx_pass(acc, lhsT, lhsT_scale, rhs, rhs_scale):
+            nc.tensor.matmul_mx(
+                out=acc, lhsT=lhsT, lhsT_scale=lhsT_scale, rhs=rhs, rhs_scale=rhs_scale, start=True, stop=True
+            )
 
-        def shared_second(name, c0, width):
-            acc_shared[name] = shared_bank[:, c0 : c0 + width]
-            second_layer(name, SHARED, width, acc_shared[name])
+        def interleaving_activation(dst, bank, func):
+            nc.scalar.activation(dst.rearrange("p (c t) -> p c t", t=PACK), bank.rearrange("p t c -> p c t"), func)
 
-        def routed_first(name, e, c0, width):
-            first_layer(name, e, xgw[e][:, c0 : c0 + width], xgs[e][:, c0 : c0 + width], width)
+        def turned_relu(piece, e):
+            relu[piece] = tile([P, C // BLOCK, PACK, P], F32, "relu_" + piece)
+            for block in range(C // BLOCK):
+                cols = slice(block * BLOCK, (block + 1) * BLOCK)
+                acc = psum1.tile([P, H], F32, name="bank1")
+                mx_pass(
+                    acc[:], slot_words[e][:, cols].bitcast(FP8X4), slot_scales[e][:, cols], w1w[e].bitcast(FP4X4), w1s[:, e, :]
+                )
+                nc.scalar.activation(relu[piece][:, block], acc[:].rearrange("p (m t) -> p t m", t=PACK), ACT.Relu)
 
-        def routed_second(name, e, c0, width, on_vector):
-            acc = ps2.tile([P, width], F32, name="acc2")
-            second_layer(name, e, width, acc[:])
-            slots = y[:, e * C + c0 : e * C + c0 + width]
-            if on_vector:
-                nc.vector.tensor_copy(slots, acc[:])
-            else:
-                nc.scalar.copy(slots, acc[:])
+        def turned_square(piece):
+            hidden[piece] = tile([P, C * PACK], BF16, "hidden_" + piece)
+            for block in range(C // BLOCK):
+                turned = psum1.tile([P, PACK, BLOCK], F32, name="bank1")
+                for t in range(PACK):
+                    nc.tensor.transpose(turned[:, t, :], relu[piece][:, block, t, :], ident[:])
+                interleaving_activation(hidden[piece][:, block * H : (block + 1) * H], turned[:], ACT.Square)
 
-        def fetch(which, c0, width):
-            picked = tile([P, width], F32, "picked%d_%d" % (which, c0))
-            lists = (pos1_sb, pos2_sb)[which][:, c0 // 16 : (c0 + width) // 16]
-            nc.vector.tensor_tensor(picked[:], y[:].indirect(lists), gates[:, which, c0 : c0 + width], ALU.mult)
+        def permuted_relu(piece, e, words, scales):
+            width = scales.shape[1]
+            relu[piece] = tile([P, width * PACK], F32, "relu_" + piece)
+            for block in range(width // BLOCK):
+                cols = slice(block * BLOCK, (block + 1) * BLOCK)
+                acc = psum1.tile([P, PACK, BLOCK], F32, name="bank1")
+                for t in range(PACK):
+                    mx_pass(
+                        acc[:, t, :],
+                        perm_words[e][:, 2 * P * t : 2 * P * (t + 1)].bitcast(FP4X4),
+                        perm_scales[e][:, P * t : P * (t + 1)],
+                        words[:, cols].bitcast(FP8X4),
+                        scales[:, cols],
+                    )
+                interleaving_activation(relu[piece][:, block * H : (block + 1) * H], acc[:], ACT.Relu)
+
+        def square_on_vector(piece):
+            hidden[piece] = tile(list(relu[piece][:].shape), BF16, "hidden_" + piece)
+            nc.vector.tensor_tensor(hidden[piece][:], relu[piece][:], relu[piece][:], ALU.mult)
+
+        def square_on_scalar(piece):
+            hidden[piece] = tile(list(relu[piece][:].shape), BF16, "hidden_" + piece)
+            nc.scalar.activation(hidden[piece][:], relu[piece][:], ACT.Square)
+
+        def second_layer(piece, e):
+            width = hidden[piece][:].shape[1] // PACK
+            acc = psum2.tile([P, width], F32, name="bank2")
+            words = tile([P, width], U32, "h_words_" + piece)
+            scales = tile([P, width], U8, "h_scales_" + piece)
+            nc.vector.quantize_mx(out=words[:].bitcast(FP8X4), scales=scales[:], in_=hidden[piece][:])
+            mx_pass(acc[:], w2w[:, e, :].bitcast(FP4X4), w2s[:, e, :], words[:].bitcast(FP8X4), scales[:])
+            return acc
+
+        def fetch(positions, which):
+            picked = tile([P, T], F32, "picked%d" % which)
+            nc.vector.tensor_tensor(picked[:], y[:].indirect(positions[:]), gates[:, which, :], ALU.mult)
             return picked
 
-        def finish(name, c0, width):
-            total = tile([P, width], F32, "total_%s" % name)
-            nc.vector.tensor_tensor(total[:], acc_shared[name], routed[:, c0 : c0 + width], ALU.add)
-            nc.sync.dma_start(out[:, c0 : c0 + width], total[:])
-
-        gather_words(0)
-        permute_w1(SHARED)
-        shared_first("s0", 0, C)
         gather_scales(0)
+        gather_words(0)
         gather_words(1)
-        turned_first("e0", 0, [nc.scalar, nc.scalar])
+        turned_relu("e0", 0)
         gather_scales(1)
-        turned_first("e1", 1, [nc.scalar, nc.vector])
+        turned_relu("e1", 1)
         turned_square("e0")
         gather_words(2)
         gather_scales(2)
         permute_w1(2)
-        routed_first("e2", 2, 0, C)
+        permuted_relu("e2", 2, slot_words[2][:], slot_scales[2][:])
         turned_square("e1")
         gather_words(3)
         gather_scales(3)
         permute_w1(3)
-        routed_first("e3a", 3, 0, COLS)
-        routed_first("e3b", 3, COLS, COLS)
-        square("e2", C, [nc.vector])
-        square("e3a", COLS, [nc.vector])
-        square("e3b", COLS, [nc.scalar])
-        routed_second("e0", 0, 0, C, False)
-        routed_second("e1", 1, 0, C, False)
-        routed_second("e2", 2, 0, C, False)
-        routed_second("e3a", 3, 0, COLS, False)
-        routed_second("e3b", 3, COLS, COLS, True)
-        square("s0", C, [nc.scalar])
-        shared_second("s0", 0, C)
-        shared_first("s1", C, C)
-        square("s1", C, [nc.scalar])
-        a = fetch(0, 0, T)
-        b = fetch(1, 0, T)
-        shared_second("s1", C, C)
-        routed = tile([P, T], F32, "hid_s1")
-        nc.vector.tensor_tensor(routed[:], a[:], b[:], ALU.add)
-        finish("s0", 0, C)
-        finish("s1", C, C)
+        permuted_relu("e3a", 3, slot_words[3][:, :BLOCK], slot_scales[3][:, :BLOCK])
+        permuted_relu("e3b", 3, slot_words[3][:, BLOCK:], slot_scales[3][:, BLOCK:])
+        for piece in ("e2", "e3a", "e3b"):
+            square_on_vector(piece)
+        permute_w1(SHARED)
+        for e in range(E - 1):
+            nc.scalar.copy(y[:, e * C : (e + 1) * C], second_layer("e%d" % e, e)[:])
+        nc.scalar.copy(y[:, SLOTS - C : SLOTS - BLOCK], second_layer("e3a", 3)[:])
+        nc.vector.tensor_copy(y[:, SLOTS - BLOCK :], second_layer("e3b", 3)[:])
+
+        permuted_relu("s0", SHARED, xw[:, :HALF], xs[:, :HALF])
+        square_on_scalar("s0")
+        shared0 = second_layer("s0", SHARED)
+        permuted_relu("s1", SHARED, xw[:, HALF:], xs[:, HALF:])
+        square_on_scalar("s1")
+        picked = [fetch(pos1_sb, 0), fetch(pos2_sb, 1)]
+        shared1 = second_layer("s1", SHARED)
+        routed = tile([P, T], F32, "hidden_s1")
+        nc.vector.tensor_tensor(routed[:], picked[0][:], picked[1][:], ALU.add)
+        for half, shared in enumerate((shared0, shared1)):
+            cols = slice(half * HALF, (half + 1) * HALF)
+            total = tile([P, HALF], F32, "total%d" % half)
+            nc.vector.tensor_tensor(total[:], shared[:], routed[:, cols], ALU.add)
+            nc.sync.dma_start(out[:, cols], total[:])

@@ -27,6 +27,7 @@ PER_COLUMN = 16
 LINE = 16
 BLOCK = 128
 HALF = T // 2
+assert HALF == C
 TURNED = 2
 
 
@@ -117,18 +118,22 @@ def tile_moe_shr_mlp_relu2_kernel(
                 out=acc, lhsT=lhsT, lhsT_scale=lhsT_scale, rhs=rhs, rhs_scale=rhs_scale, start=True, stop=True
             )
 
-        def interleaving_activation(dst, bank, func):
-            nc.scalar.activation(dst.rearrange("p (c t) -> p c t", t=PACK), bank.rearrange("p t c -> p c t"), func)
+        def interleaved(dst, bank):
+            return dst.rearrange("p (c t) -> p c t", t=PACK), bank.rearrange("p t c -> p c t")
 
-        def turned_relu(piece, e):
+        def relu_on_scalar(dst, src):
+            nc.scalar.activation(dst, src, ACT.Relu)
+
+        def relu_on_vector(dst, src):
+            nc.vector.tensor_scalar_max(dst, src, 0.0)
+
+        def turned_relu(piece, e, words, scales):
             relu[piece] = tile([P, C // BLOCK, PACK, P], F32, "relu_" + piece)
             for block in range(C // BLOCK):
                 cols = slice(block * BLOCK, (block + 1) * BLOCK)
                 acc = psum1.tile([P, H], F32, name="bank1")
-                mx_pass(
-                    acc[:], slot_words[e][:, cols].bitcast(FP8X4), slot_scales[e][:, cols], w1w[e].bitcast(FP4X4), w1s[:, e, :]
-                )
-                nc.scalar.activation(relu[piece][:, block], acc[:].rearrange("p (m t) -> p t m", t=PACK), ACT.Relu)
+                mx_pass(acc[:], words[:, cols].bitcast(FP8X4), scales[:, cols], w1w[e].bitcast(FP4X4), w1s[:, e, :])
+                relu_on_scalar(relu[piece][:, block], acc[:].rearrange("p (m t) -> p t m", t=PACK))
 
         def turned_square(piece):
             hidden[piece] = tile([P, C * PACK], BF16, "hidden_" + piece)
@@ -136,36 +141,31 @@ def tile_moe_shr_mlp_relu2_kernel(
                 turned = psum1.tile([P, PACK, BLOCK], F32, name="bank1")
                 for t in range(PACK):
                     nc.tensor.transpose(turned[:, t, :], relu[piece][:, block, t, :], ident[:])
-                interleaving_activation(hidden[piece][:, block * H : (block + 1) * H], turned[:], ACT.Square)
+                nc.scalar.activation(*interleaved(hidden[piece][:, block * H : (block + 1) * H], turned[:]), ACT.Square)
 
-        def permuted_relu(piece, e, words, scales):
-            width = scales.shape[1]
-            relu[piece] = tile([P, width * PACK], F32, "relu_" + piece)
-            for block in range(width // BLOCK):
-                cols = slice(block * BLOCK, (block + 1) * BLOCK)
+        def permuted_relu(piece, e, first_slot, block_relus):
+            relu[piece] = tile([P, len(block_relus) * H], F32, "relu_" + piece)
+            for block, block_relu in enumerate(block_relus):
+                cols = slice(first_slot + block * BLOCK, first_slot + (block + 1) * BLOCK)
                 acc = psum1.tile([P, PACK, BLOCK], F32, name="bank1")
                 for t in range(PACK):
                     mx_pass(
                         acc[:, t, :],
                         perm_words[e][:, 2 * P * t : 2 * P * (t + 1)].bitcast(FP4X4),
                         perm_scales[e][:, P * t : P * (t + 1)],
-                        words[:, cols].bitcast(FP8X4),
-                        scales[:, cols],
+                        slot_words[e][:, cols].bitcast(FP8X4),
+                        slot_scales[e][:, cols],
                     )
-                interleaving_activation(relu[piece][:, block * H : (block + 1) * H], acc[:], ACT.Relu)
+                block_relu(*interleaved(relu[piece][:, block * H : (block + 1) * H], acc[:]))
 
-        def square_on_vector(piece):
+        def permuted_square(piece):
             hidden[piece] = tile(list(relu[piece][:].shape), BF16, "hidden_" + piece)
             nc.vector.tensor_tensor(hidden[piece][:], relu[piece][:], relu[piece][:], ALU.mult)
 
-        def square_on_scalar(piece):
-            hidden[piece] = tile(list(relu[piece][:].shape), BF16, "hidden_" + piece)
-            nc.scalar.activation(hidden[piece][:], relu[piece][:], ACT.Square)
-
-        def second_layer(piece, e):
+        def second_layer(piece, e, words_buffer=None):
             width = hidden[piece][:].shape[1] // PACK
             acc = psum2.tile([P, width], F32, name="bank2")
-            words = tile([P, width], U32, "h_words_" + piece)
+            words = tile([P, width], U32, words_buffer or "h_words_" + piece)
             scales = tile([P, width], U8, "h_scales_" + piece)
             nc.vector.quantize_mx(out=words[:].bitcast(FP8X4), scales=scales[:], in_=hidden[piece][:])
             mx_pass(acc[:], w2w[:, e, :].bitcast(FP4X4), w2s[:, e, :], words[:].bitcast(FP8X4), scales[:])
@@ -179,34 +179,33 @@ def tile_moe_shr_mlp_relu2_kernel(
         gather_scales(0)
         gather_words(0)
         gather_words(1)
-        turned_relu("e0", 0)
+        turned_relu("e0", 0, slot_words[0][:], slot_scales[0][:])
         gather_scales(1)
-        turned_relu("e1", 1)
+        turned_relu("e1", 1, slot_words[1][:], slot_scales[1][:])
         turned_square("e0")
         gather_words(2)
         gather_scales(2)
         permute_w1(2)
-        permuted_relu("e2", 2, slot_words[2][:], slot_scales[2][:])
+        permuted_relu("e2", 2, 0, [relu_on_scalar, relu_on_vector])
         turned_square("e1")
         gather_words(3)
         gather_scales(3)
         permute_w1(3)
-        permuted_relu("e3a", 3, slot_words[3][:, :BLOCK], slot_scales[3][:, :BLOCK])
-        permuted_relu("e3b", 3, slot_words[3][:, BLOCK:], slot_scales[3][:, BLOCK:])
+        permuted_relu("e3a", 3, 0, [relu_on_scalar])
+        permuted_relu("e3b", 3, BLOCK, [relu_on_scalar])
         for piece in ("e2", "e3a", "e3b"):
-            square_on_vector(piece)
-        permute_w1(SHARED)
+            permuted_square(piece)
         for e in range(E - 1):
             nc.scalar.copy(y[:, e * C : (e + 1) * C], second_layer("e%d" % e, e)[:])
-        nc.scalar.copy(y[:, SLOTS - C : SLOTS - BLOCK], second_layer("e3a", 3)[:])
+        nc.vector.tensor_copy(y[:, SLOTS - C : SLOTS - BLOCK], second_layer("e3a", 3)[:])
         nc.vector.tensor_copy(y[:, SLOTS - BLOCK :], second_layer("e3b", 3)[:])
 
-        permuted_relu("s0", SHARED, xw[:, :HALF], xs[:, :HALF])
-        square_on_scalar("s0")
-        shared0 = second_layer("s0", SHARED)
-        permuted_relu("s1", SHARED, xw[:, HALF:], xs[:, HALF:])
-        square_on_scalar("s1")
+        turned_relu("s0", SHARED, xw[:, :HALF], xs[:, :HALF])
+        turned_relu("s1", SHARED, xw[:, HALF:], xs[:, HALF:])
+        turned_square("s0")
+        turned_square("s1")
         picked = [fetch(pos1_sb, 0), fetch(pos2_sb, 1)]
+        shared0 = second_layer("s0", SHARED, "relu_s1")
         shared1 = second_layer("s1", SHARED)
         routed = tile([P, T], F32, "hidden_s1")
         nc.vector.tensor_tensor(routed[:], picked[0][:], picked[1][:], ALU.add)

@@ -28,7 +28,6 @@ LINE = 16
 BLOCK = 128
 HALF = T // 2
 assert HALF == C
-TURNED = 2
 
 
 def tile_moe_shr_mlp_relu2_kernel(
@@ -38,11 +37,13 @@ def tile_moe_shr_mlp_relu2_kernel(
     with ExitStack() as ctx:
         keep = ctx.enter_context(tc.tile_pool(name="keep", bufs=1))
         ring = ctx.enter_context(tc.tile_pool(name="ring", bufs=2))
-        psum1 = ctx.enter_context(tc.psum_pool(name="psum1", bufs=5))
-        psum2 = ctx.enter_context(tc.psum_pool(name="psum2", bufs=3))
+        psum = ctx.enter_context(tc.psum_pool(name="psum", bufs=1))
 
-        def tile(shape, dtype, name, pool=keep):
-            return pool.tile(shape, dtype, name=name, align_bytes=64)
+        def tile(shape, dtype, name):
+            return keep.tile(shape, dtype, name=name, align_bytes=64)
+
+        def bank(number, shape):
+            return psum.tile(shape, F32, name="bank%d" % number)
 
         xw = tile([P, T], U32, "xw")
         xs = tile([P, T], U8, "xs")
@@ -73,33 +74,40 @@ def tile_moe_shr_mlp_relu2_kernel(
             for r in range(LIVE):
                 nc.sync.dma_start(plane[r:P:QUAD].bitcast(I32), rows[r].bitcast(I32))
 
+        def load_token_scales():
+            x_rows = x_scales[0].rearrange("(q r) t -> q r t", r=LIVE).bitcast(I32)
+            for q in range(P // QUAD):
+                repeated = x_rows[q].unsqueeze(0).broadcast_to([QUAD // LIVE, LIVE, T // 4])
+                nc.sync.dma_start(xs[QUAD * q : QUAD * (q + 1), :].bitcast(I32), repeated)
+
+        def load_token_words():
+            nc.sync.dma_start(xw[:].bitcast(I32), x_words[0].rearrange("p t r -> p (t r)").bitcast(I32))
+
         nc.sync.dma_start(offs_sb[:], offs)
-        x_rows = x_scales[0].rearrange("(q r) t -> q r t", r=LIVE).bitcast(I32)
-        for q in range(P // QUAD):
-            repeated = x_rows[q].unsqueeze(0).broadcast_to([QUAD // LIVE, LIVE, T // 4])
-            nc.sync.dma_start(xs[QUAD * q : QUAD * (q + 1), :].bitcast(I32), repeated)
-        nc.sync.dma_start(xw[:].bitcast(I32), x_words[0].rearrange("p t r -> p (t r)").bitcast(I32))
-        load_w1_words(0, TURNED)
+        load_token_scales()
+        load_token_words()
+        load_w1_words(0, 2)
         load_weight_scales(w1s[:], w1_scales)
-        load_w1_words(TURNED, E + 1)
+        load_w1_words(2, E + 1)
         nc.sync.dma_start(w2w[:].bitcast(I32), w2_words[:, 0].rearrange("e p b -> p e b").bitcast(I32))
         load_weight_scales(w2s[:], w2_scales)
         nc.sync.dma_start(pos1_sb[:], pos1)
         nc.sync.dma_start(pos2_sb[:], pos2)
         nc.sync.dma_start(gates[:], gate.rearrange("g p t -> p g t"))
 
-        slot_words, slot_scales, perm_words, perm_scales, relu, hidden = {}, {}, {}, {}, {}, {}
+        col_words, col_scales, perm_words, perm_scales, relu, hidden, sums = {}, {}, {}, {}, {}, {}, {}
+        col_words[SHARED], col_scales[SHARED] = xw, xs
 
         def expert_entries(e):
             return offs_sb[:, e * C // PER_COLUMN : (e + 1) * C // PER_COLUMN]
 
         def gather_words(e):
-            slot_words[e] = tile([P, C], U32, "slot_words", ring)
-            nc.vector.tensor_copy(slot_words[e][:], xw[:].indirect(expert_entries(e)))
+            col_words[e] = tile([P, C], U32, "slot_words%d" % e)
+            nc.vector.tensor_copy(col_words[e][:], xw[:].indirect(expert_entries(e)))
 
         def gather_scales(e):
-            slot_scales[e] = tile([P, C], U8, "slot_scales", ring)
-            nc.vector.tensor_copy(slot_scales[e][:], xs[:].indirect(expert_entries(e)))
+            col_scales[e] = ring.tile([P, C], U8, name="slot_scales", align_bytes=64)
+            nc.vector.tensor_copy(col_scales[e][:], xs[:].indirect(expert_entries(e)))
 
         def reorder(dst, src, run):
             nc.vector.tensor_copy(
@@ -108,9 +116,9 @@ def tile_moe_shr_mlp_relu2_kernel(
             )
 
         def permute_w1(e):
-            perm_words[e] = tile([P, 2 * H], U8, "perm_words", ring)
+            perm_words[e] = tile([P, 2 * H], U8, "perm_words%d" % e)
             reorder(perm_words[e][:].bitcast(U16), w1w[e].bitcast(U16), LINE // 2)
-            perm_scales[e] = tile([P, H], U8, "perm_scales", ring)
+            perm_scales[e] = tile([P, H], U8, "perm_scales%d" % e)
             reorder(perm_scales[e][:], w1s[:, e, :], LINE)
 
         def mx_pass(acc, lhsT, lhsT_scale, rhs, rhs_scale):
@@ -118,99 +126,193 @@ def tile_moe_shr_mlp_relu2_kernel(
                 out=acc, lhsT=lhsT, lhsT_scale=lhsT_scale, rhs=rhs, rhs_scale=rhs_scale, start=True, stop=True
             )
 
-        def interleaved(dst, bank):
-            return dst.rearrange("p (c t) -> p c t", t=PACK), bank.rearrange("p t c -> p c t")
+        def interleaved(dst, src):
+            return dst.rearrange("p (c t) -> p c t", t=PACK), src.rearrange("p t c -> p c t")
 
-        def relu_on_scalar(dst, src):
-            nc.scalar.activation(dst, src, ACT.Relu)
+        def relu_on(engine, dst, src):
+            if engine is nc.scalar:
+                nc.scalar.activation(dst, src, ACT.Relu)
+            else:
+                nc.vector.tensor_scalar_max(dst, src, 0.0)
 
-        def relu_on_vector(dst, src):
-            nc.vector.tensor_scalar_max(dst, src, 0.0)
+        def copy_on(engine, dst, src):
+            if engine is nc.scalar:
+                nc.scalar.copy(dst, src)
+            else:
+                nc.vector.tensor_copy(dst, src)
 
-        def turned_relu(piece, e, words, scales):
-            relu[piece] = tile([P, C // BLOCK, PACK, P], F32, "relu_" + piece)
-            for block in range(C // BLOCK):
-                cols = slice(block * BLOCK, (block + 1) * BLOCK)
-                acc = psum1.tile([P, H], F32, name="bank1")
-                mx_pass(acc[:], words[:, cols].bitcast(FP8X4), scales[:, cols], w1w[e].bitcast(FP4X4), w1s[:, e, :])
-                relu_on_scalar(relu[piece][:, block], acc[:].rearrange("p (m t) -> p t m", t=PACK))
+        def hidden_block(e, b):
+            if (e, b // 2) not in hidden:
+                hidden[e, b // 2] = tile([P, 2 * H], BF16, "hidden%d_%d" % (e, b // 2))
+            return hidden[e, b // 2][:, (b % 2) * H : (b % 2 + 1) * H]
 
-        def turned_square(piece):
-            hidden[piece] = tile([P, C * PACK], BF16, "hidden_" + piece)
-            for block in range(C // BLOCK):
-                turned = psum1.tile([P, PACK, BLOCK], F32, name="bank1")
-                for t in range(PACK):
-                    nc.tensor.transpose(turned[:, t, :], relu[piece][:, block, t, :], ident[:])
-                nc.scalar.activation(*interleaved(hidden[piece][:, block * H : (block + 1) * H], turned[:]), ACT.Square)
+        def turned_product(e, b, number):
+            cols = slice(b * BLOCK, (b + 1) * BLOCK)
+            sums[e, b] = bank(number, [P, H])
+            mx_pass(
+                sums[e, b][:],
+                col_words[e][:, cols].bitcast(FP8X4),
+                col_scales[e][:, cols],
+                w1w[e].bitcast(FP4X4),
+                w1s[:, e, :],
+            )
 
-        def permuted_relu(piece, e, first_slot, block_relus):
-            relu[piece] = tile([P, len(block_relus) * H], F32, "relu_" + piece)
-            for block, block_relu in enumerate(block_relus):
-                cols = slice(first_slot + block * BLOCK, first_slot + (block + 1) * BLOCK)
-                acc = psum1.tile([P, PACK, BLOCK], F32, name="bank1")
-                for t in range(PACK):
-                    mx_pass(
-                        acc[:, t, :],
-                        perm_words[e][:, 2 * P * t : 2 * P * (t + 1)].bitcast(FP4X4),
-                        perm_scales[e][:, P * t : P * (t + 1)],
-                        slot_words[e][:, cols].bitcast(FP8X4),
-                        slot_scales[e][:, cols],
-                    )
-                block_relu(*interleaved(relu[piece][:, block * H : (block + 1) * H], acc[:]))
+        def relu_buffer(e, blocks, name):
+            shared = tile([P, len(blocks), PACK, P], F32, name)
+            for place, b in enumerate(blocks):
+                relu[e, b] = shared[:, place]
 
-        def permuted_square(piece):
-            hidden[piece] = tile(list(relu[piece][:].shape), BF16, "hidden_" + piece)
-            nc.vector.tensor_tensor(hidden[piece][:], relu[piece][:], relu[piece][:], ALU.mult)
+        def turned_relu(e, b, engine):
+            if (e, b) not in relu:
+                relu_buffer(e, [b], "relu%d_%d" % (e, b))
+            relu_on(engine, relu[e, b], sums[e, b][:].rearrange("p (m t) -> p t m", t=PACK))
 
-        def second_layer(piece, e, words_buffer=None):
-            width = hidden[piece][:].shape[1] // PACK
-            acc = psum2.tile([P, width], F32, name="bank2")
-            words = tile([P, width], U32, words_buffer or "h_words_" + piece)
-            scales = tile([P, width], U8, "h_scales_" + piece)
-            nc.vector.quantize_mx(out=words[:].bitcast(FP8X4), scales=scales[:], in_=hidden[piece][:])
-            mx_pass(acc[:], w2w[:, e, :].bitcast(FP4X4), w2s[:, e, :], words[:].bitcast(FP8X4), scales[:])
-            return acc
+        def turn(e, b, number):
+            sums[e, b] = bank(number, [P, PACK, BLOCK])
+            for t in range(PACK):
+                nc.tensor.transpose(sums[e, b][:, t, :], relu[e, b][:, t, :], ident[:])
 
-        def fetch(positions, which):
-            picked = tile([P, T], F32, "picked%d" % which)
-            nc.vector.tensor_tensor(picked[:], y[:].indirect(positions[:]), gates[:, which, :], ALU.mult)
+        def turned_square(e, b):
+            nc.scalar.activation(*interleaved(hidden_block(e, b), sums[e, b][:]), ACT.Square)
+
+        def permuted_product(e, b, number):
+            cols = slice(b * BLOCK, (b + 1) * BLOCK)
+            sums[e, b] = bank(number, [P, PACK, BLOCK])
+            for t in range(PACK):
+                mx_pass(
+                    sums[e, b][:, t, :],
+                    perm_words[e][:, 2 * P * t : 2 * P * (t + 1)].bitcast(FP4X4),
+                    perm_scales[e][:, P * t : P * (t + 1)],
+                    col_words[e][:, cols].bitcast(FP8X4),
+                    col_scales[e][:, cols],
+                )
+
+        def permuted_relu(e, b, engine):
+            relu[e, b] = tile([P, H], F32, "relu%d_%d" % (e, b))
+            relu_on(engine, *interleaved(relu[e, b][:], sums[e, b][:]))
+
+        def permuted_square(e, b, engine):
+            if engine is nc.scalar:
+                nc.scalar.activation(hidden_block(e, b), relu[e, b][:], ACT.Square)
+            else:
+                nc.vector.tensor_tensor(hidden_block(e, b), relu[e, b][:], relu[e, b][:], ALU.mult)
+
+        codes = {}
+
+        def quantize(e, first, blocks, buffer=None):
+            source = hidden[e, first // 2][:] if blocks == 2 else hidden_block(e, first)
+            words = tile([P, blocks * BLOCK], U32, buffer or "h_words%d_%d" % (e, first))
+            scales = tile([P, blocks * BLOCK], U8, "h_scales%d_%d" % (e, first))
+            nc.vector.quantize_mx(out=words[:].bitcast(FP8X4), scales=scales[:], in_=source)
+            codes[e, first] = words, scales
+
+        def second_product(e, first, number):
+            words, scales = codes[e, first]
+            sums[e, first] = bank(number, list(words[:].shape))
+            mx_pass(sums[e, first][:], w2w[:, e, :].bitcast(FP4X4), w2s[:, e, :], words[:].bitcast(FP8X4), scales[:])
+
+        def keep_results(e, first, engine):
+            start = e * C + first * BLOCK
+            copy_on(engine, y[:, start : start + sums[e, first][:].shape[1]], sums[e, first][:])
+
+        def fetch(positions, which, first, width, buffer=None):
+            picked = tile([P, width], F32, buffer or "picked%d_%d" % (which, first))
+            entries = positions[:, first // PER_COLUMN : (first + width) // PER_COLUMN]
+            nc.vector.tensor_tensor(picked[:], y[:].indirect(entries), gates[:, which, first : first + width], ALU.mult)
             return picked
 
+        def add(name, a, b):
+            total = tile(list(b.shape), F32, name)
+            nc.vector.tensor_tensor(total[:], a, b, ALU.add)
+            return total
+
+        V, S = nc.vector, nc.scalar
         gather_scales(0)
+        gather_scales(1)
         gather_words(0)
         gather_words(1)
-        turned_relu("e0", 0, slot_words[0][:], slot_scales[0][:])
-        gather_scales(1)
-        turned_relu("e1", 1, slot_words[1][:], slot_scales[1][:])
-        turned_square("e0")
         gather_words(2)
+        gather_words(3)
+        turned_product(0, 0, 0)
+        turned_product(0, 1, 1)
         gather_scales(2)
         permute_w1(2)
-        permuted_relu("e2", 2, 0, [relu_on_scalar, relu_on_vector])
-        turned_square("e1")
-        gather_words(3)
+        turned_product(1, 0, 2)
+        turned_product(1, 1, 3)
         gather_scales(3)
         permute_w1(3)
-        permuted_relu("e3a", 3, 0, [relu_on_scalar])
-        permuted_relu("e3b", 3, BLOCK, [relu_on_scalar])
-        for piece in ("e2", "e3a", "e3b"):
-            permuted_square(piece)
-        for e in range(E - 1):
-            nc.scalar.copy(y[:, e * C : (e + 1) * C], second_layer("e%d" % e, e)[:])
-        nc.vector.tensor_copy(y[:, SLOTS - C : SLOTS - BLOCK], second_layer("e3a", 3)[:])
-        nc.vector.tensor_copy(y[:, SLOTS - BLOCK :], second_layer("e3b", 3)[:])
-
-        turned_relu("s0", SHARED, xw[:, :HALF], xs[:, :HALF])
-        turned_relu("s1", SHARED, xw[:, HALF:], xs[:, HALF:])
-        turned_square("s0")
-        turned_square("s1")
-        picked = [fetch(pos1_sb, 0), fetch(pos2_sb, 1)]
-        shared0 = second_layer("s0", SHARED, "relu_s1")
-        shared1 = second_layer("s1", SHARED)
-        routed = tile([P, T], F32, "hidden_s1")
-        nc.vector.tensor_tensor(routed[:], picked[0][:], picked[1][:], ALU.add)
-        for half, shared in enumerate((shared0, shared1)):
-            cols = slice(half * HALF, (half + 1) * HALF)
-            total = tile([P, HALF], F32, "total%d" % half)
-            nc.vector.tensor_tensor(total[:], shared[:], routed[:, cols], ALU.add)
-            nc.sync.dma_start(out[:, cols], total[:])
+        turned_relu(0, 0, S)
+        turned_relu(0, 1, S)
+        turned_relu(1, 0, S)
+        turned_relu(1, 1, S)
+        turn(0, 0, 4)
+        turn(0, 1, 0)
+        turn(1, 0, 1)
+        turn(1, 1, 2)
+        turned_square(0, 0)
+        turned_square(0, 1)
+        permuted_product(2, 0, 3)
+        permuted_product(2, 1, 4)
+        permuted_product(3, 0, 0)
+        turned_square(1, 0)
+        permuted_product(3, 1, 1)
+        permuted_relu(2, 0, V)
+        permuted_relu(2, 1, V)
+        quantize(0, 0, 2)
+        turned_square(1, 1)
+        permuted_relu(3, 0, V)
+        second_product(0, 0, 2)
+        quantize(1, 0, 2)
+        permuted_square(2, 0, S)
+        permuted_relu(3, 1, S)
+        permuted_square(2, 1, S)
+        permuted_square(3, 0, V)
+        turned_product(4, 1, 0)
+        second_product(1, 0, 5)
+        permuted_square(3, 1, S)
+        quantize(2, 0, 2)
+        turned_product(4, 0, 1)
+        quantize(3, 0, 1, "relu2_1")
+        quantize(3, 1, 1)
+        keep_results(0, 0, S)
+        keep_results(1, 0, S)
+        second_product(2, 0, 6)
+        second_product(3, 0, 7)
+        second_product(3, 1, 3)
+        turned_product(4, 2, 2)
+        turned_product(4, 3, 5)
+        relu_buffer(4, [0, 1], "relu3_1")
+        turned_relu(4, 0, V)
+        turned_relu(4, 1, V)
+        keep_results(2, 0, S)
+        keep_results(3, 0, S)
+        keep_results(3, 1, S)
+        relu_buffer(4, [2, 3], "h_words3_1")
+        turned_relu(4, 2, S)
+        turned_relu(4, 3, S)
+        turn(4, 0, 4)
+        turn(4, 1, 0)
+        turn(4, 2, 1)
+        turn(4, 3, 6)
+        picked0a = fetch(pos1_sb, 0, 0, HALF)
+        picked1a = fetch(pos2_sb, 1, 0, HALF)
+        picked0b = fetch(pos1_sb, 0, HALF, HALF)
+        routed_a = add("routed_a", picked0a[:], picked1a[:])
+        picked1b = fetch(pos2_sb, 1, HALF, HALF)
+        turned_square(4, 0)
+        turned_square(4, 1)
+        quantize(4, 0, 2)
+        turned_square(4, 2)
+        second_product(4, 0, 7)
+        quantize(4, 2, 1)
+        routed_b = add("hidden4_0", picked0b[:], picked1b[:])
+        turned_square(4, 3)
+        quantize(4, 3, 1)
+        second_product(4, 2, 3)
+        second_product(4, 3, 2)
+        total = add("hidden4_1", sums[4, 0][:], routed_a[:, 0:256])
+        nc.sync.dma_start(out[:, 0:256], total[:])
+        total = add("total2", sums[4, 2][:], routed_b[:, 0:128])
+        nc.sync.dma_start(out[:, 256:384], total[:])
+        total = add("total3", sums[4, 3][:], routed_b[:, 128:256])
+        nc.sync.dma_start(out[:, 384:512], total[:])

@@ -27,6 +27,7 @@ PER_COLUMN = 16
 LINE = 16
 BLOCK = 128
 HALF = T // 2
+FIRST = 2
 assert HALF == C
 
 
@@ -47,7 +48,9 @@ def tile_moe_shr_mlp_relu2_kernel(
 
         xw = tile([P, T], U32, "xw")
         xs = tile([P, T], U8, "xs")
-        w1s = tile([P, E + 1, H], U8, "w1s")
+        w1s_first = tile([P, FIRST, H], U8, "w1s_first")
+        w1s_rest = tile([P, E + 1 - FIRST, H], U8, "w1s_rest")
+        w1s = [w1s_first[:, e, :] if e < FIRST else w1s_rest[:, e - FIRST, :] for e in range(E + 1)]
         w2s = tile([P, E + 1, N], U8, "w2s")
         w2w = tile([P, E + 1, 2 * N], U8, "w2w")
         offs_sb = tile([P, SLOTS // PER_COLUMN], U16, "offs_sb")
@@ -57,7 +60,7 @@ def tile_moe_shr_mlp_relu2_kernel(
         ident = tile([P, P], F32, "ident")
         y = tile([P, SLOTS], F32, "y")
 
-        for plane in (w1s, w2s):
+        for plane in (w1s_first, w1s_rest, w2s):
             nc.vector.memset(plane[:].rearrange("p e c -> p (e c)").bitcast(I32), 0)
         make_identity(nc, ident[:])
 
@@ -86,11 +89,14 @@ def tile_moe_shr_mlp_relu2_kernel(
         nc.sync.dma_start(offs_sb[:], offs)
         load_token_scales()
         load_token_words()
-        load_w1_words(0, 2)
-        load_weight_scales(w1s[:], w1_scales)
-        load_w1_words(2, E + 1)
+        load_w1_words(0, FIRST)
+        load_weight_scales(w1s_first[:], w1_scales[:FIRST])
+        load_weight_scales(w1s_rest[:], w1_scales[FIRST:])
+        load_w1_words(2, 3)
+        load_w1_words(3, 4)
         nc.sync.dma_start(w2w[:].bitcast(I32), w2_words[:, 0].rearrange("e p b -> p e b").bitcast(I32))
         load_weight_scales(w2s[:], w2_scales)
+        load_w1_words(SHARED, E + 1)
         nc.sync.dma_start(pos1_sb[:], pos1)
         nc.sync.dma_start(pos2_sb[:], pos2)
         nc.sync.dma_start(gates[:], gate.rearrange("g p t -> p g t"))
@@ -119,7 +125,7 @@ def tile_moe_shr_mlp_relu2_kernel(
             perm_words[e] = tile([P, 2 * H], U8, "perm_words%d" % e)
             reorder(perm_words[e][:].bitcast(U16), w1w[e].bitcast(U16), LINE // 2)
             perm_scales[e] = tile([P, H], U8, "perm_scales%d" % e)
-            reorder(perm_scales[e][:], w1s[:, e, :], LINE)
+            reorder(perm_scales[e][:], w1s[e], LINE)
 
         def mx_pass(acc, lhsT, lhsT_scale, rhs, rhs_scale):
             nc.tensor.matmul_mx(
@@ -154,7 +160,7 @@ def tile_moe_shr_mlp_relu2_kernel(
                 col_words[e][:, cols].bitcast(FP8X4),
                 col_scales[e][:, cols],
                 w1w[e].bitcast(FP4X4),
-                w1s[:, e, :],
+                w1s[e],
             )
 
         def relu_buffer(e, blocks, name):

@@ -27,7 +27,7 @@ PER_COLUMN = 16
 LINE = 16
 BLOCK = 128
 HALF = T // 2
-FIRST = 2
+FIRST = 3
 assert HALF == C
 
 
@@ -92,8 +92,7 @@ def tile_moe_shr_mlp_relu2_kernel(
         load_w1_words(0, FIRST)
         load_weight_scales(w1s_first[:], w1_scales[:FIRST])
         load_weight_scales(w1s_rest[:], w1_scales[FIRST:])
-        load_w1_words(2, 3)
-        load_w1_words(3, 4)
+        load_w1_words(FIRST, E)
         nc.sync.dma_start(w2w[:].bitcast(I32), w2_words[:, 0].rearrange("e p b -> p e b").bitcast(I32))
         load_weight_scales(w2s[:], w2_scales)
         load_w1_words(SHARED, E + 1)
@@ -115,17 +114,17 @@ def tile_moe_shr_mlp_relu2_kernel(
             col_scales[e] = ring.tile([P, C], U8, name="slot_scales", align_bytes=64)
             nc.vector.tensor_copy(col_scales[e][:], xs[:].indirect(expert_entries(e)))
 
-        def reorder(dst, src, run):
-            nc.vector.tensor_copy(
+        def reorder(engine, dst, src, run):
+            engine.tensor_copy(
                 dst.rearrange("p (t a b) -> p a t b", t=PACK, b=run),
                 src.rearrange("p (a b t) -> p a t b", t=PACK, b=run),
             )
 
-        def permute_w1(e):
+        def permute_w1(e, words_on=nc.vector, scales_on=nc.vector):
             perm_words[e] = tile([P, 2 * H], U8, "perm_words%d" % e)
-            reorder(perm_words[e][:].bitcast(U16), w1w[e].bitcast(U16), LINE // 2)
+            reorder(words_on, perm_words[e][:].bitcast(U16), w1w[e].bitcast(U16), LINE // 2)
             perm_scales[e] = tile([P, H], U8, "perm_scales%d" % e)
-            reorder(perm_scales[e][:], w1s[e], LINE)
+            reorder(scales_on, perm_scales[e][:], w1s[e], LINE)
 
         def mx_pass(acc, lhsT, lhsT_scale, rhs, rhs_scale):
             nc.tensor.matmul_mx(
@@ -151,6 +150,12 @@ def tile_moe_shr_mlp_relu2_kernel(
             if (e, b // 2) not in hidden:
                 hidden[e, b // 2] = tile([P, 2 * H], BF16, "hidden%d_%d" % (e, b // 2))
             return hidden[e, b // 2][:, (b % 2) * H : (b % 2 + 1) * H]
+
+        def warm_up(passes, number):
+            idle = bank(number, [P, H])
+            for i in range(passes):
+                cols = slice(i * BLOCK, (i + 1) * BLOCK)
+                mx_pass(idle[:], xw[:, cols].bitcast(FP8X4), xs[:, cols], xw[:, :HALF].bitcast(FP4X4), xs[:])
 
         def turned_product(e, b, number):
             cols = slice(b * BLOCK, (b + 1) * BLOCK)
@@ -201,7 +206,7 @@ def tile_moe_shr_mlp_relu2_kernel(
             if engine is nc.scalar:
                 nc.scalar.activation(hidden_block(e, b), relu[e, b][:], ACT.Square)
             else:
-                nc.vector.tensor_tensor(hidden_block(e, b), relu[e, b][:], relu[e, b][:], ALU.mult)
+                engine.tensor_tensor(hidden_block(e, b), relu[e, b][:], relu[e, b][:], ALU.mult)
 
         codes = {}
 
@@ -232,7 +237,14 @@ def tile_moe_shr_mlp_relu2_kernel(
             nc.vector.tensor_tensor(total[:], a, b, ALU.add)
             return total
 
+        def finish(total, first, routed):
+            cols = slice(first * BLOCK, first * BLOCK + routed.shape[1])
+            nc.vector.tensor_tensor(total[:, cols], sums[SHARED, first][:], routed, ALU.add)
+            nc.sync.dma_start(out[:, cols], total[:, cols])
+
+        G = nc.gpsimd
         V, S = nc.vector, nc.scalar
+        warm_up(2, 7)
         gather_scales(0)
         gather_scales(1)
         gather_words(0)
@@ -242,64 +254,64 @@ def tile_moe_shr_mlp_relu2_kernel(
         turned_product(0, 0, 0)
         turned_product(0, 1, 1)
         gather_scales(2)
-        permute_w1(2)
+        permute_w1(2, G, G)
         turned_product(1, 0, 2)
         turned_product(1, 1, 3)
         gather_scales(3)
-        permute_w1(3)
+        permute_w1(3, G, G)
         turned_relu(0, 0, S)
         turned_relu(0, 1, S)
         turned_relu(1, 0, S)
         turned_relu(1, 1, S)
         turn(0, 0, 4)
-        turn(0, 1, 0)
-        turn(1, 0, 1)
-        turn(1, 1, 2)
+        turn(0, 1, 5)
+        permuted_product(2, 0, 1)
+        permuted_product(2, 1, 2)
+        turn(1, 0, 0)
+        turn(1, 1, 3)
         turned_square(0, 0)
+        permuted_product(3, 0, 4)
         turned_square(0, 1)
-        permuted_product(2, 0, 3)
-        permuted_product(2, 1, 4)
-        permuted_product(3, 0, 0)
-        turned_square(1, 0)
-        permuted_product(3, 1, 1)
+        permuted_product(3, 1, 5)
         permuted_relu(2, 0, V)
         permuted_relu(2, 1, V)
-        quantize(0, 0, 2)
-        turned_square(1, 1)
         permuted_relu(3, 0, V)
-        second_product(0, 0, 2)
+        quantize(0, 0, 2)
+        turned_square(1, 0)
+        turned_square(1, 1)
+        permuted_relu(3, 1, V)
+        second_product(0, 0, 6)
         quantize(1, 0, 2)
         permuted_square(2, 0, S)
-        permuted_relu(3, 1, S)
         permuted_square(2, 1, S)
-        permuted_square(3, 0, V)
-        turned_product(4, 1, 0)
-        second_product(1, 0, 5)
-        permuted_square(3, 1, S)
+        permuted_square(3, 0, S)
+        permuted_square(3, 1, V)
+        turned_product(4, 0, 0)
+        turned_product(4, 1, 3)
+        second_product(1, 0, 7)
         quantize(2, 0, 2)
-        turned_product(4, 0, 1)
-        quantize(3, 0, 1, "relu2_1")
         quantize(3, 1, 1)
+        quantize(3, 0, 1)
         keep_results(0, 0, S)
         keep_results(1, 0, S)
-        second_product(2, 0, 6)
-        second_product(3, 0, 7)
-        second_product(3, 1, 3)
-        turned_product(4, 2, 2)
-        turned_product(4, 3, 5)
-        relu_buffer(4, [0, 1], "relu3_1")
+        second_product(2, 0, 1)
+        second_product(3, 1, 4)
+        second_product(3, 0, 2)
+        turned_product(4, 2, 6)
+        turned_product(4, 3, 7)
+        relu_buffer(4, [0, 1], "relu3_0")
         turned_relu(4, 0, V)
         turned_relu(4, 1, V)
         keep_results(2, 0, S)
-        keep_results(3, 0, S)
         keep_results(3, 1, S)
-        relu_buffer(4, [2, 3], "h_words3_1")
+        keep_results(3, 0, S)
+        relu_buffer(4, [2, 3], "h_words3_0")
         turned_relu(4, 2, S)
         turned_relu(4, 3, S)
-        turn(4, 0, 4)
         turn(4, 1, 0)
-        turn(4, 2, 1)
-        turn(4, 3, 6)
+        turn(4, 0, 5)
+        turn(4, 2, 3)
+        turn(4, 3, 1)
         picked0a = fetch(pos1_sb, 0, 0, HALF)
         picked1a = fetch(pos2_sb, 1, 0, HALF)
         picked0b = fetch(pos1_sb, 0, HALF, HALF)
@@ -309,16 +321,12 @@ def tile_moe_shr_mlp_relu2_kernel(
         turned_square(4, 1)
         quantize(4, 0, 2)
         turned_square(4, 2)
-        second_product(4, 0, 7)
-        quantize(4, 2, 1)
-        routed_b = add("hidden4_0", picked0b[:], picked1b[:])
         turned_square(4, 3)
-        quantize(4, 3, 1)
-        second_product(4, 2, 3)
-        second_product(4, 3, 2)
-        total = add("hidden4_1", sums[4, 0][:], routed_a[:, 0:256])
-        nc.sync.dma_start(out[:, 0:256], total[:])
-        total = add("total2", sums[4, 2][:], routed_b[:, 0:128])
-        nc.sync.dma_start(out[:, 256:384], total[:])
-        total = add("total3", sums[4, 3][:], routed_b[:, 128:256])
-        nc.sync.dma_start(out[:, 384:512], total[:])
+        second_product(4, 0, 7)
+        quantize(4, 2, 2)
+        second_product(4, 2, 4)
+        total = tile([P, T + HALF], F32, "hidden4_1")
+        routed_b = total[:, T:]
+        nc.vector.tensor_tensor(routed_b, picked0b[:], picked1b[:], ALU.add)
+        finish(total, 0, routed_a[:, 0:256])
+        finish(total, 2, routed_b[:, 0:256])

@@ -73,9 +73,9 @@ def tile_moe_shr_mlp_relu2_kernel(
                 w1w[e] = words[:, e - first, :]
 
         def load_weight_scales(plane, scales):
-            rows = scales.rearrange("e s (q r) c -> r q (e s) c", r=LIVE)
+            rows = scales.bitcast(I32).rearrange("e s (q r) c -> r q (e s) c", r=LIVE)
             for r in range(LIVE):
-                nc.sync.dma_start(plane[r:P:QUAD].bitcast(I32), rows[r].bitcast(I32))
+                nc.sync.dma_start(plane[r:P:QUAD].bitcast(I32), rows[r])
 
         def load_token_scales():
             x_rows = x_scales[0].rearrange("(q r) t -> q r t", r=LIVE).bitcast(I32)
@@ -288,16 +288,17 @@ def tile_moe_shr_mlp_relu2_kernel(
         permuted_square(3, 1, V)
         turned_product(4, 0, 0)
         turned_product(4, 1, 3)
+        turned_product(4, 2, 5)
         second_product(1, 0, 7)
         quantize(2, 0, 2)
         quantize(3, 1, 1)
         quantize(3, 0, 1)
         keep_results(0, 0, S)
         keep_results(1, 0, S)
+        turned_relu(4, 2, S)
         second_product(2, 0, 1)
         second_product(3, 1, 4)
         second_product(3, 0, 2)
-        turned_product(4, 2, 6)
         turned_product(4, 3, 7)
         relu_buffer(4, [0, 1], "relu3_0")
         turned_relu(4, 0, V)
@@ -305,11 +306,10 @@ def tile_moe_shr_mlp_relu2_kernel(
         keep_results(2, 0, S)
         keep_results(3, 1, S)
         keep_results(3, 0, S)
-        relu_buffer(4, [2, 3], "h_words3_0")
-        turned_relu(4, 2, S)
+        relu_buffer(4, [3], "h_words3_0")
         turned_relu(4, 3, S)
+        turn(4, 0, 6)
         turn(4, 1, 0)
-        turn(4, 0, 5)
         turn(4, 2, 3)
         turn(4, 3, 1)
         picked0a = fetch(pos1_sb, 0, 0, HALF)
@@ -322,7 +322,7 @@ def tile_moe_shr_mlp_relu2_kernel(
         quantize(4, 0, 2)
         turned_square(4, 2)
         turned_square(4, 3)
-        second_product(4, 0, 7)
+        second_product(4, 0, 5)
         quantize(4, 2, 2)
         second_product(4, 2, 4)
         total = tile([P, T + HALF], F32, "hidden4_1")

@@ -262,55 +262,55 @@ def tile_moe_shr_mlp_relu2_kernel(
         turned_relu(0, 0, S)
         turned_relu(0, 1, S)
         turned_relu(1, 0, S)
-        turned_relu(1, 1, S)
+        turned_relu(1, 1, V)
         turn(0, 0, 4)
         turn(0, 1, 5)
         permuted_product(2, 0, 1)
         permuted_product(2, 1, 2)
         turn(1, 0, 0)
-        turn(1, 1, 3)
         turned_square(0, 0)
-        permuted_product(3, 0, 4)
+        turn(1, 1, 4)
+        permuted_product(3, 0, 3)
         turned_square(0, 1)
         permuted_product(3, 1, 5)
         permuted_relu(2, 0, V)
         permuted_relu(2, 1, V)
+        permuted_square(2, 0, G)
         permuted_relu(3, 0, V)
-        quantize(0, 0, 2)
         turned_square(1, 0)
-        turned_square(1, 1)
         permuted_relu(3, 1, V)
+        quantize(0, 0, 2, "perm_words3")
+        turned_product(4, 0, 0)
+        turned_square(1, 1)
+        turned_product(4, 1, 4)
+        turned_product(4, 2, 5)
         second_product(0, 0, 6)
         quantize(1, 0, 2)
-        permuted_square(2, 0, S)
         permuted_square(2, 1, S)
         permuted_square(3, 0, S)
-        permuted_square(3, 1, V)
-        turned_product(4, 0, 0)
-        turned_product(4, 1, 3)
-        turned_product(4, 2, 5)
+        permuted_square(3, 1, S)
         second_product(1, 0, 7)
         quantize(2, 0, 2)
-        quantize(3, 1, 1)
         quantize(3, 0, 1)
+        quantize(3, 1, 1)
         keep_results(0, 0, S)
         keep_results(1, 0, S)
-        turned_relu(4, 2, S)
         second_product(2, 0, 1)
-        second_product(3, 1, 4)
         second_product(3, 0, 2)
+        second_product(3, 1, 3)
         turned_product(4, 3, 7)
-        relu_buffer(4, [0, 1], "relu3_0")
+        relu_buffer(4, [0, 1], "relu3_1")
         turned_relu(4, 0, V)
         turned_relu(4, 1, V)
         keep_results(2, 0, S)
-        keep_results(3, 1, S)
         keep_results(3, 0, S)
-        relu_buffer(4, [3], "h_words3_0")
+        keep_results(3, 1, S)
+        relu_buffer(4, [2, 3], "h_words3_1")
+        turned_relu(4, 2, S)
         turned_relu(4, 3, S)
         turn(4, 0, 6)
         turn(4, 1, 0)
-        turn(4, 2, 3)
+        turn(4, 2, 4)
         turn(4, 3, 1)
         picked0a = fetch(pos1_sb, 0, 0, HALF)
         picked1a = fetch(pos2_sb, 1, 0, HALF)
@@ -324,7 +324,7 @@ def tile_moe_shr_mlp_relu2_kernel(
         turned_square(4, 3)
         second_product(4, 0, 5)
         quantize(4, 2, 2)
-        second_product(4, 2, 4)
+        second_product(4, 2, 3)
         total = tile([P, T + HALF], F32, "hidden4_1")
         routed_b = total[:, T:]
         nc.vector.tensor_tensor(routed_b, picked0b[:], picked1b[:], ALU.add)

@@ -321,12 +321,14 @@ def tile_moe_shr_mlp_relu2_kernel(
         turned_square(4, 1)
         quantize(4, 0, 2)
         turned_square(4, 2)
-        turned_square(4, 3)
         second_product(4, 0, 5)
-        quantize(4, 2, 2)
+        routed_b = add("hidden4_0", picked0b[:], picked1b[:])
+        quantize(4, 2, 1)
+        turned_square(4, 3)
+        quantize(4, 3, 1)
         second_product(4, 2, 3)
-        total = tile([P, T + HALF], F32, "hidden4_1")
-        routed_b = total[:, T:]
-        nc.vector.tensor_tensor(routed_b, picked0b[:], picked1b[:], ALU.add)
+        second_product(4, 3, 2)
+        total = tile([P, T], F32, "hidden4_1")
         finish(total, 0, routed_a[:, 0:256])
-        finish(total, 2, routed_b[:, 0:256])
+        finish(total, 2, routed_b[:, 0:128])
+        finish(total, 3, routed_b[:, 128:256])

@@ -27,7 +27,7 @@ PER_COLUMN = 16
 LINE = 16
 BLOCK = 128
 HALF = T // 2
-FIRST = 3
+FIRST = 2
 assert HALF == C
 
 
@@ -86,13 +86,13 @@ def tile_moe_shr_mlp_relu2_kernel(
         def load_token_words():
             nc.sync.dma_start(xw[:].bitcast(I32), x_words[0].rearrange("p t r -> p (t r)").bitcast(I32))
 
-        nc.sync.dma_start(offs_sb[:], offs)
         load_token_scales()
+        nc.sync.dma_start(offs_sb[:], offs)
         load_token_words()
         load_w1_words(0, FIRST)
         load_weight_scales(w1s_first[:], w1_scales[:FIRST])
-        load_weight_scales(w1s_rest[:], w1_scales[FIRST:])
         load_w1_words(FIRST, E)
+        load_weight_scales(w1s_rest[:], w1_scales[FIRST:])
         nc.sync.dma_start(w2w[:].bitcast(I32), w2_words[:, 0].rearrange("e p b -> p e b").bitcast(I32))
         load_weight_scales(w2s[:], w2_scales)
         load_w1_words(SHARED, E + 1)
@@ -221,6 +221,15 @@ def tile_moe_shr_mlp_relu2_kernel(
             words, scales = codes[e, first]
             sums[e, first] = bank(number, list(words[:].shape))
             mx_pass(sums[e, first][:], w2w[:, e, :].bitcast(FP4X4), w2s[:, e, :], words[:].bitcast(FP8X4), scales[:])
+
+        def joint_products(pieces, number):
+            widths = [codes[piece][0][:].shape[1] for piece in pieces]
+            acc = bank(number, [P, sum(widths)])
+            for place, (e, first) in enumerate(pieces):
+                words, scales = codes[e, first]
+                cols = slice(sum(widths[:place]), sum(widths[: place + 1]))
+                mx_pass(acc[:, cols], w2w[:, e, :].bitcast(FP4X4), w2s[:, e, :], words[:].bitcast(FP8X4), scales[:])
+            sums[pieces[0]] = acc
 
         def keep_results(e, first, engine):
             start = e * C + first * BLOCK

@@ -37,7 +37,6 @@ def tile_moe_shr_mlp_relu2_kernel(
     nc = tc.nc
     with ExitStack() as ctx:
         keep = ctx.enter_context(tc.tile_pool(name="keep", bufs=1))
-        ring = ctx.enter_context(tc.tile_pool(name="ring", bufs=2))
         psum = ctx.enter_context(tc.psum_pool(name="psum", bufs=1))
 
         def tile(shape, dtype, name):
@@ -48,9 +47,9 @@ def tile_moe_shr_mlp_relu2_kernel(
 
         xw = tile([P, T], U32, "xw")
         xs = tile([P, T], U8, "xs")
-        w1s_first = tile([P, FIRST, H], U8, "w1s_first")
-        w1s_rest = tile([P, E + 1 - FIRST, H], U8, "w1s_rest")
-        w1s = [w1s_first[:, e, :] if e < FIRST else w1s_rest[:, e - FIRST, :] for e in range(E + 1)]
+        w1s_first = tile([P, E, H], U8, "w1s_first")
+        w1s_rest = tile([P, 1, H], U8, "w1s_rest")
+        w1s = [w1s_first[:, e, :] if e < E else w1s_rest[:, 0, :] for e in range(E + 1)]
         w2s = tile([P, E + 1, N], U8, "w2s")
         w2w = tile([P, E + 1, 2 * N], U8, "w2w")
         offs_sb = tile([P, SLOTS // PER_COLUMN], U16, "offs_sb")
@@ -66,8 +65,8 @@ def tile_moe_shr_mlp_relu2_kernel(
 
         w1w = {}
 
-        def load_w1_words(first, last):
-            words = tile([P, last - first, 2 * H], U8, "w1w_from%d" % first)
+        def load_w1_words(first, last, buffer=None):
+            words = tile([P, last - first, 2 * H], U8, buffer or "w1w_from%d" % first)
             nc.sync.dma_start(words[:].bitcast(I32), w1_words[first:last, 0].rearrange("e p b -> p e b").bitcast(I32))
             for e in range(first, last):
                 w1w[e] = words[:, e - first, :]
@@ -90,9 +89,9 @@ def tile_moe_shr_mlp_relu2_kernel(
         nc.sync.dma_start(offs_sb[:], offs)
         load_token_words()
         load_w1_words(0, FIRST)
-        load_weight_scales(w1s_first[:], w1_scales[:FIRST])
+        load_weight_scales(w1s_first[:], w1_scales[:E])
         load_w1_words(FIRST, E)
-        load_weight_scales(w1s_rest[:], w1_scales[FIRST:])
+        load_weight_scales(w1s_rest[:], w1_scales[E:])
         nc.sync.dma_start(w2w[:].bitcast(I32), w2_words[:, 0].rearrange("e p b -> p e b").bitcast(I32))
         load_weight_scales(w2s[:], w2_scales)
         load_w1_words(SHARED, E + 1)
@@ -110,9 +109,15 @@ def tile_moe_shr_mlp_relu2_kernel(
             col_words[e] = tile([P, C], U32, "slot_words%d" % e)
             nc.vector.tensor_copy(col_words[e][:], xw[:].indirect(expert_entries(e)))
 
+        def scale_buffer(experts, name):
+            shared = tile([P, len(experts), C], U8, name)
+            for place, e in enumerate(experts):
+                col_scales[e] = shared[:, place, :]
+
         def gather_scales(e):
-            col_scales[e] = ring.tile([P, C], U8, name="slot_scales", align_bytes=64)
-            nc.vector.tensor_copy(col_scales[e][:], xs[:].indirect(expert_entries(e)))
+            if e not in col_scales:
+                scale_buffer([e], "slot_scales%d" % e)
+            nc.vector.tensor_copy(col_scales[e], xs[:].indirect(expert_entries(e)))
 
         def reorder(engine, dst, src, run):
             engine.tensor_copy(
@@ -145,6 +150,9 @@ def tile_moe_shr_mlp_relu2_kernel(
                 nc.scalar.copy(dst, src)
             else:
                 nc.vector.tensor_copy(dst, src)
+
+        def hidden_buffer(e, pair, name):
+            hidden[e, pair] = tile([P, 2 * H], BF16, name)
 
         def hidden_block(e, b):
             if (e, b // 2) not in hidden:
@@ -262,39 +270,40 @@ def tile_moe_shr_mlp_relu2_kernel(
         gather_words(3)
         turned_product(0, 0, 0)
         turned_product(0, 1, 1)
-        gather_scales(2)
+        permute_w1(1, G, G)
         permute_w1(2, G, G)
-        turned_product(1, 0, 2)
-        turned_product(1, 1, 3)
-        gather_scales(3)
         permute_w1(3, G, G)
+        scale_buffer([2, 3], "slot_scales0")
+        gather_scales(2)
+        gather_scales(3)
+        permuted_product(1, 0, 2)
+        permuted_product(1, 1, 3)
         turned_relu(0, 0, S)
         turned_relu(0, 1, S)
-        turned_relu(1, 0, S)
-        turned_relu(1, 1, V)
+        permuted_relu(1, 0, S)
+        permuted_relu(1, 1, V)
         turn(0, 0, 4)
         turn(0, 1, 5)
-        permuted_product(2, 0, 1)
-        permuted_product(2, 1, 2)
-        turn(1, 0, 0)
+        permuted_product(2, 0, 0)
+        permuted_product(2, 1, 1)
+        permuted_product(3, 0, 2)
+        permuted_product(3, 1, 3)
+        hidden_buffer(1, 0, "w1w_from2")
+        permuted_square(1, 1, G)
         turned_square(0, 0)
-        turn(1, 1, 4)
-        permuted_product(3, 0, 3)
         turned_square(0, 1)
-        permuted_product(3, 1, 5)
+        permuted_square(1, 0, S)
         permuted_relu(2, 0, V)
         permuted_relu(2, 1, V)
-        permuted_square(2, 0, G)
         permuted_relu(3, 0, V)
-        turned_square(1, 0)
         permuted_relu(3, 1, V)
+        turned_product(4, 0, 4)
+        turned_product(4, 1, 2)
+        turned_product(4, 2, 3)
         quantize(0, 0, 2, "perm_words3")
-        turned_product(4, 0, 0)
-        turned_square(1, 1)
-        turned_product(4, 1, 4)
-        turned_product(4, 2, 5)
+        quantize(1, 0, 2, "perm_scales3")
         second_product(0, 0, 6)
-        quantize(1, 0, 2)
+        permuted_square(2, 0, S)
         permuted_square(2, 1, S)
         permuted_square(3, 0, S)
         permuted_square(3, 1, S)
@@ -305,8 +314,8 @@ def tile_moe_shr_mlp_relu2_kernel(
         keep_results(0, 0, S)
         keep_results(1, 0, S)
         second_product(2, 0, 1)
-        second_product(3, 0, 2)
-        second_product(3, 1, 3)
+        second_product(3, 0, 5)
+        second_product(3, 1, 0)
         turned_product(4, 3, 7)
         relu_buffer(4, [0, 1], "relu3_1")
         turned_relu(4, 0, V)
@@ -318,8 +327,8 @@ def tile_moe_shr_mlp_relu2_kernel(
         turned_relu(4, 2, S)
         turned_relu(4, 3, S)
         turn(4, 0, 6)
-        turn(4, 1, 0)
-        turn(4, 2, 4)
+        turn(4, 1, 4)
+        turn(4, 2, 2)
         turn(4, 3, 1)
         picked0a = fetch(pos1_sb, 0, 0, HALF)
         picked1a = fetch(pos2_sb, 1, 0, HALF)
@@ -330,13 +339,13 @@ def tile_moe_shr_mlp_relu2_kernel(
         turned_square(4, 1)
         quantize(4, 0, 2)
         turned_square(4, 2)
-        second_product(4, 0, 5)
+        second_product(4, 0, 3)
         routed_b = add("hidden4_0", picked0b[:], picked1b[:])
         quantize(4, 2, 1)
         turned_square(4, 3)
         quantize(4, 3, 1)
-        second_product(4, 2, 3)
-        second_product(4, 3, 2)
+        second_product(4, 2, 5)
+        second_product(4, 3, 0)
         total = tile([P, T], F32, "hidden4_1")
         finish(total, 0, routed_a[:, 0:256])
         finish(total, 2, routed_b[:, 0:128])

@@ -80,7 +80,8 @@ def tile_moe_shr_mlp_relu2_kernel(
             x_rows = x_scales[0].rearrange("(q r) t -> q r t", r=LIVE).bitcast(I32)
             for q in range(P // QUAD):
                 repeated = x_rows[q].unsqueeze(0).broadcast_to([QUAD // LIVE, LIVE, T // 4])
-                nc.sync.dma_start(xs[QUAD * q : QUAD * (q + 1), :].bitcast(I32), repeated)
+                queue = nc.sync if q % 2 == 0 else nc.scalar
+                queue.dma_start(xs[QUAD * q : QUAD * (q + 1), :].bitcast(I32), repeated)
 
         def load_token_words():
             nc.sync.dma_start(xw[:].bitcast(I32), x_words[0].rearrange("p t r -> p (t r)").bitcast(I32))
@@ -114,22 +115,33 @@ def tile_moe_shr_mlp_relu2_kernel(
             for place, e in enumerate(experts):
                 col_scales[e] = shared[:, place, :]
 
+        def gather_scale_block(e, b):
+            block_scales[e, b] = tile([P, BLOCK], U8, "block_scales%d_%d" % (e, b))
+            first = (e * C + b * BLOCK) // PER_COLUMN
+            entries = offs_sb[:, first : first + BLOCK // PER_COLUMN]
+            nc.vector.tensor_copy(block_scales[e, b][:], xs[:].indirect(entries))
+
+        block_scales = {}
+
         def gather_scales(e):
             if e not in col_scales:
                 scale_buffer([e], "slot_scales%d" % e)
             nc.vector.tensor_copy(col_scales[e], xs[:].indirect(expert_entries(e)))
 
         def reorder(engine, dst, src, run):
-            engine.tensor_copy(
+            move = nc.scalar.copy if engine is nc.scalar else engine.tensor_copy
+            move(
                 dst.rearrange("p (t a b) -> p a t b", t=PACK, b=run),
                 src.rearrange("p (a b t) -> p a t b", t=PACK, b=run),
             )
 
-        def permute_w1(e, words_on=nc.vector, scales_on=nc.vector):
+        def permute_words(e, engine):
             perm_words[e] = tile([P, 2 * H], U8, "perm_words%d" % e)
-            reorder(words_on, perm_words[e][:].bitcast(U16), w1w[e].bitcast(U16), LINE // 2)
+            reorder(engine, perm_words[e][:].bitcast(U16), w1w[e].bitcast(U16), LINE // 2)
+
+        def permute_scales(e, engine):
             perm_scales[e] = tile([P, H], U8, "perm_scales%d" % e)
-            reorder(scales_on, perm_scales[e][:], w1s[e], LINE)
+            reorder(engine, perm_scales[e][:], w1s[e], LINE)
 
         def mx_pass(acc, lhsT, lhsT_scale, rhs, rhs_scale):
             nc.tensor.matmul_mx(
@@ -154,16 +166,32 @@ def tile_moe_shr_mlp_relu2_kernel(
         def hidden_buffer(e, pair, name):
             hidden[e, pair] = tile([P, 2 * H], BF16, name)
 
+        own_hidden = {}
+
+        def hidden_run(pieces, name):
+            shared = tile([P, len(pieces) * H], BF16, name)
+            for place, piece in enumerate(pieces):
+                own_hidden[piece] = shared[:, place * H : (place + 1) * H]
+            runs[pieces[0]] = shared, pieces
+
+        runs = {}
+
+        def quantize_run(first, buffer=None):
+            source, pieces = runs[first]
+            words = tile([P, len(pieces) * BLOCK], U32, buffer or "h_words%d_%d" % first)
+            scales = tile([P, len(pieces) * BLOCK], U8, "h_scales%d_%d" % first)
+            nc.vector.quantize_mx(out=words[:].bitcast(FP8X4), scales=scales[:], in_=source[:])
+            for place, piece in enumerate(pieces):
+                count = len([other for other in pieces[place:] if other[0] == piece[0]])
+                cols = slice(place * BLOCK, (place + count) * BLOCK)
+                codes[piece] = words[:, cols], scales[:, cols]
+
         def hidden_block(e, b):
+            if (e, b) in own_hidden:
+                return own_hidden[e, b]
             if (e, b // 2) not in hidden:
                 hidden[e, b // 2] = tile([P, 2 * H], BF16, "hidden%d_%d" % (e, b // 2))
             return hidden[e, b // 2][:, (b % 2) * H : (b % 2 + 1) * H]
-
-        def warm_up(passes, number):
-            idle = bank(number, [P, H])
-            for i in range(passes):
-                cols = slice(i * BLOCK, (i + 1) * BLOCK)
-                mx_pass(idle[:], xw[:, cols].bitcast(FP8X4), xs[:, cols], xw[:, :HALF].bitcast(FP4X4), xs[:])
 
         def turned_product(e, b, number):
             cols = slice(b * BLOCK, (b + 1) * BLOCK)
@@ -171,7 +199,7 @@ def tile_moe_shr_mlp_relu2_kernel(
             mx_pass(
                 sums[e, b][:],
                 col_words[e][:, cols].bitcast(FP8X4),
-                col_scales[e][:, cols],
+                block_scales[e, b][:] if (e, b) in block_scales else col_scales[e][:, cols],
                 w1w[e].bitcast(FP4X4),
                 w1s[e],
             )
@@ -249,10 +277,19 @@ def tile_moe_shr_mlp_relu2_kernel(
             nc.vector.tensor_tensor(picked[:], y[:].indirect(entries), gates[:, which, first : first + width], ALU.mult)
             return picked
 
+        def fetch_plain(positions, first, width, name):
+            picked = tile([P, width], F32, name)
+            entries = positions[:, first // PER_COLUMN : (first + width) // PER_COLUMN]
+            nc.scalar.activation(picked[:], y[:].indirect(entries), ACT.Copy)
+            return picked
+
+        def combine(name, a, b, op):
+            result = tile(list(b.shape), F32, name)
+            nc.vector.tensor_tensor(result[:], a, b, op)
+            return result
+
         def add(name, a, b):
-            total = tile(list(b.shape), F32, name)
-            nc.vector.tensor_tensor(total[:], a, b, ALU.add)
-            return total
+            return combine(name, a, b, ALU.add)
 
         def finish(total, first, routed):
             cols = slice(first * BLOCK, first * BLOCK + routed.shape[1])
@@ -261,8 +298,8 @@ def tile_moe_shr_mlp_relu2_kernel(
 
         G = nc.gpsimd
         V, S = nc.vector, nc.scalar
-        warm_up(2, 7)
-        gather_scales(0)
+        gather_scale_block(0, 0)
+        gather_scale_block(0, 1)
         gather_scales(1)
         gather_words(0)
         gather_words(1)
@@ -270,10 +307,13 @@ def tile_moe_shr_mlp_relu2_kernel(
         gather_words(3)
         turned_product(0, 0, 0)
         turned_product(0, 1, 1)
-        permute_w1(1, G, G)
-        permute_w1(2, G, G)
-        permute_w1(3, G, G)
-        scale_buffer([2, 3], "slot_scales0")
+        permute_words(1, G)
+        permute_scales(1, G)
+        permute_words(2, G)
+        permute_scales(2, G)
+        permute_words(3, G)
+        permute_scales(3, G)
+        scale_buffer([2, 3], "block_scales0_0")
         gather_scales(2)
         gather_scales(3)
         permuted_product(1, 0, 2)
@@ -288,11 +328,12 @@ def tile_moe_shr_mlp_relu2_kernel(
         permuted_product(2, 1, 1)
         permuted_product(3, 0, 2)
         permuted_product(3, 1, 3)
-        hidden_buffer(1, 0, "w1w_from2")
+        hidden_run([(1, 1)], "w1w_from2")
+        hidden_run([(0, 0), (0, 1), (1, 0)], "hidden0")
         permuted_square(1, 1, G)
+        permuted_square(1, 0, S)
         turned_square(0, 0)
         turned_square(0, 1)
-        permuted_square(1, 0, S)
         permuted_relu(2, 0, V)
         permuted_relu(2, 1, V)
         permuted_relu(3, 0, V)
@@ -300,14 +341,14 @@ def tile_moe_shr_mlp_relu2_kernel(
         turned_product(4, 0, 4)
         turned_product(4, 1, 2)
         turned_product(4, 2, 3)
-        quantize(0, 0, 2, "perm_words3")
-        quantize(1, 0, 2, "perm_scales3")
+        quantize_run((0, 0), "perm_words3")
+        quantize_run((1, 1), "perm_scales3")
         second_product(0, 0, 6)
         permuted_square(2, 0, S)
         permuted_square(2, 1, S)
         permuted_square(3, 0, S)
         permuted_square(3, 1, S)
-        second_product(1, 0, 7)
+        joint_products([(1, 0), (1, 1)], 7)
         quantize(2, 0, 2)
         quantize(3, 0, 1)
         quantize(3, 1, 1)

@@ -47,9 +47,9 @@ def tile_moe_shr_mlp_relu2_kernel(
 
         xw = tile([P, T], U32, "xw")
         xs = tile([P, T], U8, "xs")
-        w1s_first = tile([P, E, H], U8, "w1s_first")
-        w1s_rest = tile([P, 1, H], U8, "w1s_rest")
-        w1s = [w1s_first[:, e, :] if e < E else w1s_rest[:, 0, :] for e in range(E + 1)]
+        w1s_first = tile([P, FIRST, H], U8, "w1s_first")
+        w1s_rest = tile([P, E + 1 - FIRST, H], U8, "w1s_rest")
+        w1s = [w1s_first[:, e, :] if e < FIRST else w1s_rest[:, e - FIRST, :] for e in range(E + 1)]
         w2s = tile([P, E + 1, N], U8, "w2s")
         w2w = tile([P, E + 1, 2 * N], U8, "w2w")
         offs_sb = tile([P, SLOTS // PER_COLUMN], U16, "offs_sb")
@@ -59,43 +59,44 @@ def tile_moe_shr_mlp_relu2_kernel(
         ident = tile([P, P], F32, "ident")
         y = tile([P, SLOTS], F32, "y")
 
-        for plane in (w1s_first, w1s_rest, w2s):
-            nc.vector.memset(plane[:].rearrange("p e c -> p (e c)").bitcast(I32), 0)
+        for plane, engine in ((w1s_first, nc.vector), (w1s_rest, nc.vector), (w2s, nc.vector)):
+            engine.memset(plane[:].rearrange("p e c -> p (e c)").bitcast(I32), 0)
         make_identity(nc, ident[:])
 
         w1w = {}
 
-        def load_w1_words(first, last, buffer=None):
-            words = tile([P, last - first, 2 * H], U8, buffer or "w1w_from%d" % first)
-            nc.sync.dma_start(words[:].bitcast(I32), w1_words[first:last, 0].rearrange("e p b -> p e b").bitcast(I32))
+        def load_w1_words(first, last, queue=nc.sync):
+            words = tile([P, last - first, 2 * H], U8, "w1w_from%d" % first)
+            queue.dma_start(words[:].bitcast(I32), w1_words[first:last, 0].rearrange("e p b -> p e b").bitcast(I32))
             for e in range(first, last):
                 w1w[e] = words[:, e - first, :]
 
-        def load_weight_scales(plane, scales):
+        def load_weight_scales(plane, scales, queues=(nc.sync,) * LIVE):
             rows = scales.bitcast(I32).rearrange("e s (q r) c -> r q (e s) c", r=LIVE)
             for r in range(LIVE):
-                nc.sync.dma_start(plane[r:P:QUAD].bitcast(I32), rows[r])
+                queues[r].dma_start(plane[r:P:QUAD].bitcast(I32), rows[r])
 
-        def load_token_scales():
+        def load_token_scales(q, queue):
             x_rows = x_scales[0].rearrange("(q r) t -> q r t", r=LIVE).bitcast(I32)
-            for q in range(P // QUAD):
-                repeated = x_rows[q].unsqueeze(0).broadcast_to([QUAD // LIVE, LIVE, T // 4])
-                queue = nc.sync if q % 2 == 0 else nc.scalar
-                queue.dma_start(xs[QUAD * q : QUAD * (q + 1), :].bitcast(I32), repeated)
+            repeated = x_rows[q].unsqueeze(0).broadcast_to([QUAD // LIVE, LIVE, T // 4])
+            queue.dma_start(xs[QUAD * q : QUAD * (q + 1), :].bitcast(I32), repeated)
 
-        def load_token_words():
-            nc.sync.dma_start(xw[:].bitcast(I32), x_words[0].rearrange("p t r -> p (t r)").bitcast(I32))
+        def load_token_words(queue):
+            queue.dma_start(xw[:].bitcast(I32), x_words[0].rearrange("p t r -> p (t r)").bitcast(I32))
 
-        load_token_scales()
+        load_token_scales(0, nc.sync)
+        load_token_scales(1, nc.scalar)
+        load_token_scales(2, nc.sync)
+        load_token_scales(3, nc.scalar)
         nc.sync.dma_start(offs_sb[:], offs)
-        load_token_words()
+        load_token_words(nc.sync)
         load_w1_words(0, FIRST)
-        load_weight_scales(w1s_first[:], w1_scales[:E])
+        load_weight_scales(w1s_first[:], w1_scales[:FIRST])
         load_w1_words(FIRST, E)
-        load_weight_scales(w1s_rest[:], w1_scales[E:])
+        load_weight_scales(w1s_rest[:], w1_scales[FIRST:])
+        load_w1_words(SHARED, E + 1)
         nc.sync.dma_start(w2w[:].bitcast(I32), w2_words[:, 0].rearrange("e p b -> p e b").bitcast(I32))
         load_weight_scales(w2s[:], w2_scales)
-        load_w1_words(SHARED, E + 1)
         nc.sync.dma_start(pos1_sb[:], pos1)
         nc.sync.dma_start(pos2_sb[:], pos2)
         nc.sync.dma_start(gates[:], gate.rearrange("g p t -> p g t"))
@@ -135,8 +136,8 @@ def tile_moe_shr_mlp_relu2_kernel(
                 src.rearrange("p (a b t) -> p a t b", t=PACK, b=run),
             )
 
-        def permute_words(e, engine):
-            perm_words[e] = tile([P, 2 * H], U8, "perm_words%d" % e)
+        def permute_words(e, engine, buffer=None):
+            perm_words[e] = tile([P, 2 * H], U8, buffer or "perm_words%d" % e)
             reorder(engine, perm_words[e][:].bitcast(U16), w1w[e].bitcast(U16), LINE // 2)
 
         def permute_scales(e, engine):
@@ -311,13 +312,13 @@ def tile_moe_shr_mlp_relu2_kernel(
         permute_scales(1, G)
         permute_words(2, G)
         permute_scales(2, G)
-        permute_words(3, G)
-        permute_scales(3, G)
         scale_buffer([2, 3], "block_scales0_0")
         gather_scales(2)
         gather_scales(3)
         permuted_product(1, 0, 2)
         permuted_product(1, 1, 3)
+        permute_words(3, G, "perm_words1")
+        permute_scales(3, G)
         turned_relu(0, 0, S)
         turned_relu(0, 1, S)
         permuted_relu(1, 0, S)
@@ -341,7 +342,7 @@ def tile_moe_shr_mlp_relu2_kernel(
         turned_product(4, 0, 4)
         turned_product(4, 1, 2)
         turned_product(4, 2, 3)
-        quantize_run((0, 0), "perm_words3")
+        quantize_run((0, 0), "perm_words1")
         quantize_run((1, 1), "perm_scales3")
         second_product(0, 0, 6)
         permuted_square(2, 0, S)

@@ -27,6 +27,7 @@ PER_COLUMN = 16
 LINE = 16
 BLOCK = 128
 HALF = T // 2
+WINDOW = 704
 FIRST = 2
 assert HALF == C
 
@@ -45,8 +46,8 @@ def tile_moe_shr_mlp_relu2_kernel(
         def bank(number, shape):
             return psum.tile(shape, F32, name="bank%d" % number)
 
-        xw = tile([P, T], U32, "xw")
-        xs = tile([P, T], U8, "xs")
+        xw = tile([P, WINDOW], U32, "xw")
+        xs = tile([P, WINDOW], U8, "xs")
         w1s_first = tile([P, FIRST, H], U8, "w1s_first")
         w1s_rest = tile([P, E + 1 - FIRST, H], U8, "w1s_rest")
         w1s = [w1s_first[:, e, :] if e < FIRST else w1s_rest[:, e - FIRST, :] for e in range(E + 1)]
@@ -61,6 +62,8 @@ def tile_moe_shr_mlp_relu2_kernel(
 
         for plane, engine in ((w1s_first, nc.vector), (w1s_rest, nc.vector), (w2s, nc.vector)):
             engine.memset(plane[:].rearrange("p e c -> p (e c)").bitcast(I32), 0)
+        for table in (xs, xw):
+            nc.vector.memset(table[:, T:].bitcast(I32), 0)
         make_identity(nc, ident[:])
 
         w1w = {}
@@ -79,10 +82,10 @@ def tile_moe_shr_mlp_relu2_kernel(
         def load_token_scales(q, queue):
             x_rows = x_scales[0].rearrange("(q r) t -> q r t", r=LIVE).bitcast(I32)
             repeated = x_rows[q].unsqueeze(0).broadcast_to([QUAD // LIVE, LIVE, T // 4])
-            queue.dma_start(xs[QUAD * q : QUAD * (q + 1), :].bitcast(I32), repeated)
+            queue.dma_start(xs[QUAD * q : QUAD * (q + 1), :T].bitcast(I32), repeated)
 
         def load_token_words(queue):
-            queue.dma_start(xw[:].bitcast(I32), x_words[0].rearrange("p t r -> p (t r)").bitcast(I32))
+            queue.dma_start(xw[:, :T].bitcast(I32), x_words[0].rearrange("p t r -> p (t r)").bitcast(I32))
 
         load_token_scales(0, nc.sync)
         load_token_scales(1, nc.scalar)
@@ -110,6 +113,13 @@ def tile_moe_shr_mlp_relu2_kernel(
         def gather_words(e):
             col_words[e] = tile([P, C], U32, "slot_words%d" % e)
             nc.vector.tensor_copy(col_words[e][:], xw[:].indirect(expert_entries(e)))
+
+        def gather_experts(table, found, first, count, name):
+            picked = tile([P, count, C], table[:].dtype, name)
+            entries = offs_sb[:, first * C // PER_COLUMN : (first + count) * C // PER_COLUMN]
+            nc.vector.tensor_copy(picked[:].rearrange("p e c -> p (e c)"), table[:].indirect(entries))
+            for place in range(count):
+                found[first + place] = picked[:, place, :]
 
         def scale_buffer(experts, name):
             shared = tile([P, len(experts), C], U8, name)
@@ -299,22 +309,17 @@ def tile_moe_shr_mlp_relu2_kernel(
 
         G = nc.gpsimd
         V, S = nc.vector, nc.scalar
-        gather_scale_block(0, 0)
-        gather_scale_block(0, 1)
-        gather_scales(1)
-        gather_words(0)
-        gather_words(1)
-        gather_words(2)
-        gather_words(3)
+        gather_experts(xs, col_scales, 0, 2, "slot_scales0")
+        gather_experts(xw, col_words, 0, 1, "slot_words0")
+        gather_experts(xw, col_words, 1, 1, "slot_words1")
+        gather_experts(xw, col_words, 2, 2, "slot_words2")
         turned_product(0, 0, 0)
         turned_product(0, 1, 1)
         permute_words(1, G)
         permute_scales(1, G)
         permute_words(2, G)
         permute_scales(2, G)
-        scale_buffer([2, 3], "block_scales0_0")
-        gather_scales(2)
-        gather_scales(3)
+        gather_experts(xs, col_scales, 2, 2, "slot_words0")
         permuted_product(1, 0, 2)
         permuted_product(1, 1, 3)
         permute_words(3, G, "perm_words1")
@@ -365,30 +370,30 @@ def tile_moe_shr_mlp_relu2_kernel(
         keep_results(2, 0, S)
         keep_results(3, 0, S)
         keep_results(3, 1, S)
-        relu_buffer(4, [2, 3], "h_words3_1")
+        relu_buffer(4, [2], "h_words3_1")
+        relu_buffer(4, [3], "h_scales3_1")
         turned_relu(4, 2, S)
         turned_relu(4, 3, S)
         turn(4, 0, 6)
         turn(4, 1, 4)
         turn(4, 2, 2)
-        turn(4, 3, 1)
-        picked0a = fetch(pos1_sb, 0, 0, HALF)
-        picked1a = fetch(pos2_sb, 1, 0, HALF)
-        picked0b = fetch(pos1_sb, 0, HALF, HALF)
-        routed_a = add("routed_a", picked0a[:], picked1a[:])
-        picked1b = fetch(pos2_sb, 1, HALF, HALF)
+        picked0 = fetch(pos1_sb, 0, 0, T)
+        picked1 = fetch(pos2_sb, 1, 0, T)
         turned_square(4, 0)
+        turn(4, 3, 6)
         turned_square(4, 1)
         quantize(4, 0, 2)
         turned_square(4, 2)
         second_product(4, 0, 3)
-        routed_b = add("hidden4_0", picked0b[:], picked1b[:])
+        routed = tile([P, T], F32, "h_scales3_1")
+        V.tensor_tensor(routed[:, :HALF], picked0[:, :HALF], picked1[:, :HALF], ALU.add)
         quantize(4, 2, 1)
+        V.tensor_tensor(routed[:, HALF:], picked0[:, HALF:], picked1[:, HALF:], ALU.add)
         turned_square(4, 3)
         quantize(4, 3, 1)
         second_product(4, 2, 5)
         second_product(4, 3, 0)
-        total = tile([P, T], F32, "hidden4_1")
-        finish(total, 0, routed_a[:, 0:256])
-        finish(total, 2, routed_b[:, 0:128])
-        finish(total, 3, routed_b[:, 128:256])
+        total = tile([P, T], F32, "h_words4_2")
+        finish(total, 0, routed[:, 0:256])
+        finish(total, 2, routed[:, 256:384])
+        finish(total, 3, routed[:, 384:512])

@@ -223,7 +223,11 @@ def tile_moe_shr_mlp_relu2_kernel(
         def turned_relu(e, b, engine):
             if (e, b) not in relu:
                 relu_buffer(e, [b], "relu%d_%d" % (e, b))
-            relu_on(engine, relu[e, b], sums[e, b][:].rearrange("p (m t) -> p t m", t=PACK))
+            relu_on(
+                engine,
+                relu[e, b].rearrange("p t (a c) -> p a t c", c=PACK),
+                sums[e, b][:].rearrange("p (a c t) -> p a t c", c=PACK, t=PACK),
+            )
 
         def turn(e, b, number):
             sums[e, b] = bank(number, [P, PACK, BLOCK])

from contextlib import ExitStack

import concourse.mybir as mybir
from concourse.masks import make_identity

K, T, E, C, H, N = 512, 512, 4, 256, 512, 128
SLOTS = E * C
SHARED = E
FLOPS = 2 * (SLOTS + T) * (K * H + H * N)

F32 = mybir.dt.float32
BF16 = mybir.dt.bfloat16
I32 = mybir.dt.int32
U32 = mybir.dt.uint32
U16 = mybir.dt.uint16
U8 = mybir.dt.uint8
FP8X4 = mybir.dt.float8_e4m3fn_x4
FP4X4 = mybir.dt.float4_e2m1fn_x4
ACT = mybir.ActivationFunctionType
ALU = mybir.AluOpType

P = 128
PACK = 4
QUAD = 32
LIVE = 4
PER_COLUMN = 16
LINE = 16
BLOCK = 128
HALF = T // 2
WINDOW = 704
FIRST = 2
assert HALF == C


def tile_moe_shr_mlp_relu2_kernel(
    tc, x_words, x_scales, w1_words, w1_scales, w2_words, w2_scales, gate, offs, pos1, pos2, out
):
    nc = tc.nc
    with ExitStack() as ctx:
        keep = ctx.enter_context(tc.tile_pool(name="keep", bufs=1))
        psum = ctx.enter_context(tc.psum_pool(name="psum", bufs=1))

        def tile(shape, dtype, name):
            return keep.tile(shape, dtype, name=name, align_bytes=64)

        def bank(number, shape):
            return psum.tile(shape, F32, name="bank%d" % number)

        xw = tile([P, WINDOW], U32, "xw")
        xs = tile([P, WINDOW], U8, "xs")
        w1s_first = tile([P, FIRST, H], U8, "w1s_first")
        w1s_rest = tile([P, E + 1 - FIRST, H], U8, "w1s_rest")
        w1s = [w1s_first[:, e, :] if e < FIRST else w1s_rest[:, e - FIRST, :] for e in range(E + 1)]
        w2s = tile([P, E + 1, N], U8, "w2s")
        w2w = tile([P, E + 1, 2 * N], U8, "w2w")
        offs_sb = tile([P, SLOTS // PER_COLUMN], U16, "offs_sb")
        pos1_sb = tile([P, T // PER_COLUMN], U16, "pos1_sb")
        pos2_sb = tile([P, T // PER_COLUMN], U16, "pos2_sb")
        gates = tile([P, 2, T], F32, "gates")
        ident = tile([P, P], F32, "ident")
        y = tile([P, SLOTS], F32, "y")

        for plane, engine in ((w1s_first, nc.vector), (w1s_rest, nc.vector), (w2s, nc.vector)):
            engine.memset(plane[:].rearrange("p e c -> p (e c)").bitcast(I32), 0)
        for table in (xs, xw):
            nc.vector.memset(table[:, T:].bitcast(I32), 0)
        make_identity(nc, ident[:])

        w1w = {}

        def load_w1_words(first, last, queue=nc.sync):
            words = tile([P, last - first, 2 * H], U8, "w1w_from%d" % first)
            queue.dma_start(words[:].bitcast(I32), w1_words[first:last, 0].rearrange("e p b -> p e b").bitcast(I32))
            for e in range(first, last):
                w1w[e] = words[:, e - first, :]

        def load_weight_scales(plane, scales, queues=(nc.sync,) * LIVE):
            rows = scales.bitcast(I32).rearrange("e s (q r) c -> r q (e s) c", r=LIVE)
            for r in range(LIVE):
                queues[r].dma_start(plane[r:P:QUAD].bitcast(I32), rows[r])

        def load_token_scales(q, queue):
            x_rows = x_scales[0].rearrange("(q r) t -> q r t", r=LIVE).bitcast(I32)
            repeated = x_rows[q].unsqueeze(0).broadcast_to([QUAD // LIVE, LIVE, T // 4])
            queue.dma_start(xs[QUAD * q : QUAD * (q + 1), :T].bitcast(I32), repeated)

        def load_token_words(queue):
            queue.dma_start(xw[:, :T].bitcast(I32), x_words[0].rearrange("p t r -> p (t r)").bitcast(I32))

        load_token_scales(0, nc.sync)
        load_token_scales(1, nc.scalar)
        load_token_scales(2, nc.sync)
        load_token_scales(3, nc.scalar)
        nc.sync.dma_start(offs_sb[:], offs)
        load_token_words(nc.sync)
        load_w1_words(0, FIRST)
        load_weight_scales(w1s_first[:], w1_scales[:FIRST])
        load_w1_words(FIRST, E)
        load_weight_scales(w1s_rest[:], w1_scales[FIRST:])
        load_w1_words(SHARED, E + 1)
        nc.sync.dma_start(w2w[:].bitcast(I32), w2_words[:, 0].rearrange("e p b -> p e b").bitcast(I32))
        load_weight_scales(w2s[:], w2_scales)
        nc.sync.dma_start(pos1_sb[:], pos1)
        nc.sync.dma_start(pos2_sb[:], pos2)
        nc.sync.dma_start(gates[:], gate.rearrange("g p t -> p g t"))

        col_words, col_scales, perm_words, perm_scales, relu, hidden, sums = {}, {}, {}, {}, {}, {}, {}
        col_words[SHARED], col_scales[SHARED] = xw, xs

        def expert_entries(e):
            return offs_sb[:, e * C // PER_COLUMN : (e + 1) * C // PER_COLUMN]

        def gather_words(e):
            col_words[e] = tile([P, C], U32, "slot_words%d" % e)
            nc.vector.tensor_copy(col_words[e][:], xw[:].indirect(expert_entries(e)))

        def gather_experts(table, found, first, count, name):
            picked = tile([P, count, C], table[:].dtype, name)
            entries = offs_sb[:, first * C // PER_COLUMN : (first + count) * C // PER_COLUMN]
            nc.vector.tensor_copy(picked[:].rearrange("p e c -> p (e c)"), table[:].indirect(entries))
            for place in range(count):
                found[first + place] = picked[:, place, :]

        def scale_buffer(experts, name):
            shared = tile([P, len(experts), C], U8, name)
            for place, e in enumerate(experts):
                col_scales[e] = shared[:, place, :]

        def gather_scale_block(e, b):
            block_scales[e, b] = tile([P, BLOCK], U8, "block_scales%d_%d" % (e, b))
            first = (e * C + b * BLOCK) // PER_COLUMN
            entries = offs_sb[:, first : first + BLOCK // PER_COLUMN]
            nc.vector.tensor_copy(block_scales[e, b][:], xs[:].indirect(entries))

        block_scales = {}

        def gather_scales(e):
            if e not in col_scales:
                scale_buffer([e], "slot_scales%d" % e)
            nc.vector.tensor_copy(col_scales[e], xs[:].indirect(expert_entries(e)))

        def reorder(engine, dst, src, run):
            move = nc.scalar.copy if engine is nc.scalar else engine.tensor_copy
            move(
                dst.rearrange("p (t a b) -> p a t b", t=PACK, b=run),
                src.rearrange("p (a b t) -> p a t b", t=PACK, b=run),
            )

        def permute_words(e, engine, buffer=None):
            perm_words[e] = tile([P, 2 * H], U8, buffer or "perm_words%d" % e)
            reorder(engine, perm_words[e][:].bitcast(U16), w1w[e].bitcast(U16), LINE // 2)

        def permute_scales(e, engine):
            perm_scales[e] = tile([P, H], U8, "perm_scales%d" % e)
            reorder(engine, perm_scales[e][:], w1s[e], LINE)

        def mx_pass(acc, lhsT, lhsT_scale, rhs, rhs_scale):
            nc.tensor.matmul_mx(
                out=acc, lhsT=lhsT, lhsT_scale=lhsT_scale, rhs=rhs, rhs_scale=rhs_scale, start=True, stop=True
            )

        def interleaved(dst, src):
            return dst.rearrange("p (c t) -> p c t", t=PACK), src.rearrange("p t c -> p c t")

        def relu_on(engine, dst, src):
            if engine is nc.scalar:
                nc.scalar.activation(dst, src, ACT.Relu)
            else:
                nc.vector.tensor_scalar_max(dst, src, 0.0)

        def copy_on(engine, dst, src):
            if engine is nc.scalar:
                nc.scalar.copy(dst, src)
            else:
                nc.vector.tensor_copy(dst, src)

        def hidden_buffer(e, pair, name):
            hidden[e, pair] = tile([P, 2 * H], BF16, name)

        own_hidden = {}

        def hidden_run(pieces, name):
            shared = tile([P, len(pieces) * H], BF16, name)
            for place, piece in enumerate(pieces):
                own_hidden[piece] = shared[:, place * H : (place + 1) * H]
            runs[pieces[0]] = shared, pieces

        runs = {}

        def quantize_run(first, buffer=None):
            source, pieces = runs[first]
            words = tile([P, len(pieces) * BLOCK], U32, buffer or "h_words%d_%d" % first)
            scales = tile([P, len(pieces) * BLOCK], U8, "h_scales%d_%d" % first)
            nc.vector.quantize_mx(out=words[:].bitcast(FP8X4), scales=scales[:], in_=source[:])
            for place, piece in enumerate(pieces):
                count = len([other for other in pieces[place:] if other[0] == piece[0]])
                cols = slice(place * BLOCK, (place + count) * BLOCK)
                codes[piece] = words[:, cols], scales[:, cols]

        def hidden_block(e, b):
            if (e, b) in own_hidden:
                return own_hidden[e, b]
            if (e, b // 2) not in hidden:
                hidden[e, b // 2] = tile([P, 2 * H], BF16, "hidden%d_%d" % (e, b // 2))
            return hidden[e, b // 2][:, (b % 2) * H : (b % 2 + 1) * H]

        def turned_product(e, b, number):
            cols = slice(b * BLOCK, (b + 1) * BLOCK)
            sums[e, b] = bank(number, [P, H])
            mx_pass(
                sums[e, b][:],
                col_words[e][:, cols].bitcast(FP8X4),
                block_scales[e, b][:] if (e, b) in block_scales else col_scales[e][:, cols],
                w1w[e].bitcast(FP4X4),
                w1s[e],
            )

        def relu_buffer(e, blocks, name):
            shared = tile([P, len(blocks), PACK, P], F32, name)
            for place, b in enumerate(blocks):
                relu[e, b] = shared[:, place]

        def turned_relu(e, b, engine):
            if (e, b) not in relu:
                relu_buffer(e, [b], "relu%d_%d" % (e, b))
            relu_on(
                engine,
                relu[e, b].rearrange("p t (a c) -> p a t c", c=PACK),
                sums[e, b][:].rearrange("p (a c t) -> p a t c", c=PACK, t=PACK),
            )

        def turn(e, b, number):
            sums[e, b] = bank(number, [P, PACK, BLOCK])
            for t in range(PACK):
                nc.tensor.transpose(sums[e, b][:, t, :], relu[e, b][:, t, :], ident[:])

        def turned_square(e, b):
            nc.scalar.activation(*interleaved(hidden_block(e, b), sums[e, b][:]), ACT.Square)

        def permuted_product(e, b, number):
            cols = slice(b * BLOCK, (b + 1) * BLOCK)
            sums[e, b] = bank(number, [P, PACK, BLOCK])
            for t in range(PACK):
                mx_pass(
                    sums[e, b][:, t, :],
                    perm_words[e][:, 2 * P * t : 2 * P * (t + 1)].bitcast(FP4X4),
                    perm_scales[e][:, P * t : P * (t + 1)],
                    col_words[e][:, cols].bitcast(FP8X4),
                    col_scales[e][:, cols],
                )

        def permuted_relu(e, b, engine):
            relu[e, b] = tile([P, H], F32, "relu%d_%d" % (e, b))
            relu_on(engine, *interleaved(relu[e, b][:], sums[e, b][:]))

        def permuted_square(e, b, engine):
            if engine is nc.scalar:
                nc.scalar.activation(hidden_block(e, b), relu[e, b][:], ACT.Square)
            else:
                engine.tensor_tensor(hidden_block(e, b), relu[e, b][:], relu[e, b][:], ALU.mult)

        codes = {}

        def quantize(e, first, blocks, buffer=None):
            source = hidden[e, first // 2][:] if blocks == 2 else hidden_block(e, first)
            words = tile([P, blocks * BLOCK], U32, buffer or "h_words%d_%d" % (e, first))
            scales = tile([P, blocks * BLOCK], U8, "h_scales%d_%d" % (e, first))
            nc.vector.quantize_mx(out=words[:].bitcast(FP8X4), scales=scales[:], in_=source)
            codes[e, first] = words, scales

        def second_product(e, first, number):
            words, scales = codes[e, first]
            sums[e, first] = bank(number, list(words[:].shape))
            mx_pass(sums[e, first][:], w2w[:, e, :].bitcast(FP4X4), w2s[:, e, :], words[:].bitcast(FP8X4), scales[:])

        def joint_products(pieces, number):
            widths = [codes[piece][0][:].shape[1] for piece in pieces]
            acc = bank(number, [P, sum(widths)])
            for place, (e, first) in enumerate(pieces):
                words, scales = codes[e, first]
                cols = slice(sum(widths[:place]), sum(widths[: place + 1]))
                mx_pass(acc[:, cols], w2w[:, e, :].bitcast(FP4X4), w2s[:, e, :], words[:].bitcast(FP8X4), scales[:])
            sums[pieces[0]] = acc

        def keep_results(e, first, engine):
            start = e * C + first * BLOCK
            copy_on(engine, y[:, start : start + sums[e, first][:].shape[1]], sums[e, first][:])

        def fetch(positions, which, first, width, buffer=None):
            picked = tile([P, width], F32, buffer or "picked%d_%d" % (which, first))
            entries = positions[:, first // PER_COLUMN : (first + width) // PER_COLUMN]
            nc.vector.tensor_tensor(picked[:], y[:].indirect(entries), gates[:, which, first : first + width], ALU.mult)
            return picked

        def fetch_plain(positions, first, width, name):
            picked = tile([P, width], F32, name)
            entries = positions[:, first // PER_COLUMN : (first + width) // PER_COLUMN]
            nc.scalar.activation(picked[:], y[:].indirect(entries), ACT.Copy)
            return picked

        def combine(name, a, b, op):
            result = tile(list(b.shape), F32, name)
            nc.vector.tensor_tensor(result[:], a, b, op)
            return result

        def add(name, a, b):
            return combine(name, a, b, ALU.add)

        def finish(total, first, routed):
            cols = slice(first * BLOCK, first * BLOCK + routed.shape[1])
            nc.vector.tensor_tensor(total[:, cols], sums[SHARED, first][:], routed, ALU.add)
            nc.sync.dma_start(out[:, cols], total[:, cols])

        G = nc.gpsimd
        V, S = nc.vector, nc.scalar
        gather_experts(xs, col_scales, 0, 2, "slot_scales0")
        gather_experts(xw, col_words, 0, 1, "slot_words0")
        gather_experts(xw, col_words, 1, 1, "slot_words1")
        gather_experts(xw, col_words, 2, 2, "slot_words2")
        turned_product(0, 0, 0)
        turned_product(0, 1, 1)
        permute_words(1, G)
        permute_scales(1, G)
        permute_words(2, G)
        permute_scales(2, G)
        gather_experts(xs, col_scales, 2, 2, "slot_words0")
        permuted_product(1, 0, 2)
        permuted_product(1, 1, 3)
        permute_words(3, G, "perm_words1")
        permute_scales(3, G)
        turned_relu(0, 0, S)
        turned_relu(0, 1, S)
        permuted_relu(1, 0, S)
        permuted_relu(1, 1, V)
        turn(0, 0, 4)
        turn(0, 1, 5)
        permuted_product(2, 0, 0)
        permuted_product(2, 1, 1)
        permuted_product(3, 0, 2)
        permuted_product(3, 1, 3)
        hidden_run([(1, 1)], "w1w_from2")
        hidden_run([(0, 0), (0, 1), (1, 0)], "hidden0")
        permuted_square(1, 1, G)
        permuted_square(1, 0, S)
        turned_square(0, 0)
        turned_square(0, 1)
        permuted_relu(2, 0, V)
        permuted_relu(2, 1, V)
        permuted_relu(3, 0, V)
        permuted_relu(3, 1, V)
        turned_product(4, 0, 4)
        turned_product(4, 1, 2)
        turned_product(4, 2, 3)
        quantize_run((0, 0), "perm_words1")
        quantize_run((1, 1), "perm_scales3")
        second_product(0, 0, 6)
        permuted_square(2, 0, S)
        permuted_square(2, 1, S)
        permuted_square(3, 0, S)
        permuted_square(3, 1, S)
        joint_products([(1, 0), (1, 1)], 7)
        quantize(2, 0, 2)
        quantize(3, 0, 1)
        quantize(3, 1, 1)
        keep_results(0, 0, S)
        keep_results(1, 0, S)
        second_product(2, 0, 1)
        second_product(3, 0, 5)
        second_product(3, 1, 0)
        turned_product(4, 3, 7)
        relu_buffer(4, [0, 1], "relu3_1")
        turned_relu(4, 0, V)
        turned_relu(4, 1, V)
        keep_results(2, 0, S)
        keep_results(3, 0, S)
        keep_results(3, 1, S)
        relu_buffer(4, [2], "h_words3_1")
        relu_buffer(4, [3], "h_scales3_1")
        turned_relu(4, 2, S)
        turned_relu(4, 3, S)
        turn(4, 0, 6)
        turn(4, 1, 4)
        turn(4, 2, 2)
        picked0 = fetch(pos1_sb, 0, 0, T)
        picked1 = fetch(pos2_sb, 1, 0, T)
        turned_square(4, 0)
        turn(4, 3, 6)
        turned_square(4, 1)
        quantize(4, 0, 2)
        turned_square(4, 2)
        second_product(4, 0, 3)
        routed = tile([P, T], F32, "h_scales3_1")
        V.tensor_tensor(routed[:, :HALF], picked0[:, :HALF], picked1[:, :HALF], ALU.add)
        quantize(4, 2, 1)
        V.tensor_tensor(routed[:, HALF:], picked0[:, HALF:], picked1[:, HALF:], ALU.add)
        turned_square(4, 3)
        quantize(4, 3, 1)
        second_product(4, 2, 5)
        second_product(4, 3, 0)
        total = tile([P, T], F32, "h_words4_2")
        finish(total, 0, routed[:, 0:256])
        finish(total, 2, routed[:, 256:384])
        finish(total, 3, routed[:, 384:512])
